import numpy as np, ml_dtypes
CORES = [24,25,26,27,28,29,30,31]
N = 8
BF = ml_dtypes.bfloat16
def gentries(a):
    return np.ascontiguousarray(a.reshape(8, 16, -1).transpose(0, 2, 1)).reshape(8, -1)
def gtable(e):
    e = np.asarray(e); return np.ascontiguousarray(e.reshape(8, -1, 16).transpose(0, 2, 1)).reshape(128, -1).astype(np.int32)
W, K, Q, ST, EV = 4096, 192, 3, 4, 1
def parts(rng):
    return {"turn": np.argsort(rng.random((8, W)), axis=1), "tw": rng.integers(0, 256, (8, 16, W)), "img": rng.integers(0, W, (N, 8, K, 16)),
            "ent": rng.integers(0, W, (N, 8, Q, W)), "elen": rng.integers(0, 25, (N, 8, W)), "own": rng.integers(0, W, (N, 8, Q, K)), "olen": rng.integers(0, 25, (N, 8, K))}
def flock(rng, img, share):
    c = np.where(rng.random((N, 8, K)) < share, rng.integers(0, K, (N, 8, K)), np.arange(K))
    o = np.argsort(rng.random(img.shape), axis=3)
    return np.take_along_axis(np.take_along_axis(img, c[..., None], 2), o, 3)
def pack(p):
    return {"turn": np.tile(p["turn"][None], (N, 1, 1)).astype(np.int32), "twist": np.tile(p["tw"].reshape(1, 128, W), (N, 1, 1)).astype(np.float32).astype(BF),
            "img": np.stack([gtable(a.reshape(8, 16 * K)) for a in p["img"]]), "ent": p["ent"].reshape(N, 8, Q * W).astype(np.int32), "elen": p["elen"].astype(np.int32),
            "own": p["own"].reshape(N, 8, Q * K).astype(np.int32), "olen": p["olen"].astype(np.int32)}
def setup_inputs(rng):
    p = parts(rng); p["img"] = flock(rng, p["img"], 0.4)
    return pack(p)
def setup_inputs_crowd(rng):
    p = parts(rng); base = rng.integers(0, W, (N, 8, 3, 16)); c = rng.integers(0, 3, (N, 8, K)); c[:, ::2] = 0
    p["img"] = np.take_along_axis(base, c[..., None], 2)
    p["olen"] = 5 + rng.integers(0, 2, (N, 8, K)) * rng.integers(0, 2, (N, 8, 1)); p["elen"] = rng.integers(0, 60, (N, 8, W))
    x = np.arange(W); j = np.arange(K)
    p["elen"][:, 2::2] = rng.integers(2000, 4096, (N, 3, W))
    p["olen"][:, 2] = 3 * (K - 1 - j) + int(rng.integers(0, 100)); p["olen"][:, 6] = 3 * j + int(rng.integers(0, 100))
    two = np.argsort(rng.random((N, W)), axis=1)[:, :8 * K].reshape(N, K // 2, 16)
    p["img"][:, 4] = two[:, rng.permutation(K) % (K // 2)]; p["olen"][:, 4] = rng.integers(0, 4, (N, K))
    n = K // ST; hop = W // (ST * Q); odd = 2 * int(rng.integers(1, W // 2)) + 1; o = (x * odd + int(rng.integers(0, W))) % W
    p["turn"][5] = (x + hop * odd) % W
    s = rng.permutation(K); a = np.minimum(j // n, ST - 1)[s]; i = (j % n)[s]
    p["img"][:, 5] = np.repeat(o[(i - a * Q * hop) % W][:, None], 16, axis=1)
    p["olen"][:, 5] = 3000 - 400 * a + rng.integers(0, 200, (N, K))
    p["elen"][:, 5] = 0; p["elen"][:, 5, o[:n]] = rng.integers(3500, 4096, (N, n))
    return pack(p)
def setup_inputs_ends(rng):
    p = parts(rng); v = np.array([0, 1, W // 2, W - 1]); e = np.array([0, 1, 4094, 4095]); x = np.arange(W)
    p["turn"][0] = x; p["turn"][1] = x[::-1]; p["turn"][2] = (x + 1) % W
    p["tw"][3] = 0; p["tw"][4] = 255 * rng.integers(0, 2, (16, W)); p["tw"][5] = 255
    p["img"][:, ::2] = rng.choice(v, (N, 4, K, 16)); p["img"][:, 1] = np.repeat(p["img"][:, 1, :, :1], 16, axis=2)
    p["ent"][:, 1:5] = rng.choice(v, (N, 4, Q, W)); p["own"][:, 1:5] = rng.choice(v, (N, 4, Q, K))
    p["elen"] = rng.choice(e, (N, 8, W)); p["olen"] = rng.choice(e, (N, 8, K)); p["olen"][int(rng.integers(0, N))] = 4095
    return pack(p)
def setup_inputs_full(rng):
    p = parts(rng); hop = W // (ST * Q); x = np.arange(W); j = np.arange(K)
    for g in range(8):
        c = int(rng.integers(1, W))
        if g < 4:
            o = (16 * np.argsort(rng.random((16, W // 16)), axis=1) + rng.permutation(16)[:, None]).reshape(W)
            p["ent"][:, g] = c; p["own"][:, g] = c
        else:
            o = (x * (2 * int(rng.integers(1, W // 2)) + 1) + int(rng.integers(0, W))) % W
        sig = np.zeros(W, np.int64); sig[o] = o[(x + hop) % W]
        p["turn"][g, (x + c) % W] = (sig + c) % W
        n = K if g % 2 else min(2 * K, Q * hop); z = np.argsort(rng.random((N, n)), axis=1)
        pts = o[np.stack([z[:, :K], z[:, np.where(K + j < n, K + j, j)]], axis=2)]
        p["img"][:, g] = np.take_along_axis(pts, np.argsort(rng.random((N, K, 16)), axis=2) % 2, 2)
        p["elen"][:, g, o] = 100 * (np.minimum(x // (Q * hop), ST - 1) + 1) + rng.integers(0, 50, (N, W)); p["olen"][:, g] = rng.integers(0, 50, (N, K))
    return pack(p)
def setup_inputs_spread(rng):
    p = parts(rng)
    p["tw"] = np.minimum((np.exp2(8 * rng.random((8, 1, W))) * rng.random((8, 16, W))).astype(np.int64), 255)
    p["img"] = flock(rng, np.minimum((W * rng.random((N, 8, K, 16)) ** 3).astype(np.int64), W - 1), 0.3)
    p["ent"] = np.minimum((W * rng.random((N, 8, Q, W)) ** 2).astype(np.int64), W - 1)
    p["elen"] = np.minimum(np.exp2(12 * rng.random((N, 8, W))).astype(np.int64), 4095); p["olen"] = np.minimum(np.exp2(12 * rng.random((N, 8, K))).astype(np.int64) - 1, 4095)
    return pack(p)
def setup_inputs_ties(rng):
    p = parts(rng); o = np.argsort(rng.random((8, 16, W)), axis=1)
    p["tw"] = o % 2 * 128; p["tw"][1] = o[1]; p["tw"][5] = o[5]; p["tw"][3::4] = rng.integers(0, 4, (2, 16, W))
    p["img"] = flock(rng, p["img"], 0.7)
    low = rng.permutation(np.array([0, 0, 0, 252, 1020, 2048, 3000, 4088])).reshape(1, 8, 1)
    p["elen"] = low + rng.integers(3, 6, (N, 8, W)); p["olen"] = low + rng.integers(3, 6, (N, 8, K))
    return pack(p)
def check_inputs(d):
    bad = []
    for k, hi in (("turn", W - 1), ("img", W - 1), ("ent", W - 1), ("own", W - 1), ("elen", 4095), ("olen", 4095)):
        if np.min(d[k]) < 0 or np.max(d[k]) > hi: bad.append("range of " + k)
    t = np.asarray(d["twist"]).astype(np.float32)
    if not np.all((t >= 0) & (t <= 255) & (t == np.floor(t))): bad.append("twist: whole numbers from 0 to 255")
    if not np.all(t == t[:1]): bad.append("twist alike on all ranks")
    if not np.all(np.sort(d["turn"], axis=2) == np.arange(W)): bad.append("turn: permutations")
    if not np.all(d["turn"] == d["turn"][:1]): bad.append("turn alike on all ranks")
    return bad
def reference(turn, twist, img, ent, elen, own, olen):
    pt = turn.astype(np.int64); tw = twist.astype(np.float32).astype(np.int64).reshape(N, 8, 16, W)
    b = np.stack([gentries(a) for a in img]).astype(np.int64)
    f = np.take_along_axis(tw, b[:, :, None, :], 3)
    e = ent.astype(np.int64).reshape(N, 8, Q, W); l = elen.astype(np.int64); o = own.astype(np.int64).reshape(N, 8, Q, K); m = olen.astype(np.int64)
    ri = np.arange(N).reshape(N, 1, 1); gi = np.arange(8).reshape(1, 8, 1); big = 2 ** 40
    for step in range(1, ST + 1):
        d = np.argmax(np.add.reduce(f, axis=2).reshape(N, 8, K, 16), axis=3)
        w = np.take_along_axis(b.reshape(N, 8, K, 16), d[..., None], 3)[..., 0]
        a = np.take_along_axis(e, w[:, :, None, :], 3); al = np.take_along_axis(l, w, 2)
        for q in range(Q):
            s = np.repeat(a[:, :, q], 16, axis=2); u = (b + s) & (W - 1)
            f = (f + np.take_along_axis(tw, u[:, :, None, :], 3)) & 255
            b = (np.take_along_axis(pt, u, 2) - s) & (W - 1)
        key = np.where(m < al, m * K + np.arange(K), big); best = np.full((N, 8, W), big)
        np.minimum.at(best, (ri, gi, w), key)
        won = (m < al) & (key == np.take_along_axis(best, w, 2))
        r1, g1, j1 = np.nonzero(won); x1 = w[r1, g1, j1]
        e[r1, g1, :, x1] = o[r1, g1, :, j1]; l[r1, g1, x1] = m[r1, g1, j1]
        m = np.where(won, al, m) + Q; o = a
        if step % EV == 0: e = np.roll(e, 1, axis=0); l = np.roll(l, 1, axis=0)
    return {"yimg": np.ascontiguousarray(b.reshape(N, 8, K, 16).transpose(0, 1, 3, 2)).reshape(N, 128, K).astype(np.float32), "yf": f.reshape(N, 128, 16 * K).astype(np.float32).astype(BF),
            "yent": e.reshape(N, 8, Q * W).astype(np.float32), "yelen": l.astype(np.float32)}

@@ -1,0 +1,645 @@
+from concourse.bass import DstId, RemoteDMATransfer
+from concourse.mybir import AluOpType, AxisListType, ActivationFunctionType
+
+W, K, ST = 4096, 192, 4
+NB = 2
+LB = K // NB
+GL = 32
+TWW = W + K
+DLW = 204
+PLAIN = 4
+BK = (0, 1, 0)
+ROUNDS, VPEN, WIN, SEED, JG, JT = 8, 300.0, 100.0, 1079, 500.0, 3000.0
+DELTAS = [(s, d) for s in range(1, ST + 1) for d in range(1, ST + 2 - s)]
+
+
+def sb(n, dtype):
+    return ("sbuf", [128, n], dtype)
+
+
+SCRATCH = {}
+for _n, _c in dict(tw=W, tws=512, wv=4 * W, g0=16 * K, g1=16 * K, ff=16 * K, kk=16 * K, zb=512, mk=512, ee=12 * 194, zd=144, idb=128,
+                   n256=128, bda=2048, bdl=2048, bdb=128, zob=128, wk=8, ws=128, c15=256, one=512, eps=128, zz=194, c49=512).items():
+    SCRATCH[_n] = sb(_c, "bfloat16")
+for _n, _c in dict(w0=TWW, w1=TWW, lf=1024, tl=4096, yo=K, zr=512, rm=512, wf=12, wr=K, wn=12, sc=12 * 194, dd=194, oo=16 * 12, cc=16,
+                   ia=144, ig=128, it=128, ik=8, i32=256, ij=12, ma=16, t1=128, t2=256, t3=128, pr=128, t4=64, rs=256).items():
+    SCRATCH[_n] = sb(_c, "float32")
+for _n, _c in dict(lfi=1024, imgi=K, yi=K, ya=K, owi=K, ti=512, ci=4).items():
+    SCRATCH[_n] = sb(_c, "int32")
+for _n, _c in dict(dl=DLW * len(DELTAS), sv=DLW * ST, uu=K, wo=12).items():
+    SCRATCH[_n] = sb(_c, "uint16")
+for _n, _c in dict(bc=K, mb=K, e0=K, e1=K, tc=512, oh=24, zo=144, zl=144, idh=128, ide=128, bd=128, sd=384, wt=128).items():
+    SCRATCH[_n] = sb(_c, "float16")
+for _n in ["pf%d" % _i for _i in range(6)] + ["px0", "px1"]:
+    SCRATCH[_n] = ("psum", [128, 512], "float32")
+
+SEMAPHORES = (["sV", "sS", "sP", "sG", "rloc", "rvw"] + ["rt%d" % k for k in range(1, 5)]
+              + ["rd%d%d" % sd for sd in DELTAS] + ["q%d" % i for i in range(32)])
+
+CY, PC, GC, SCC, LAT = 1.04, 0.52, 1.62, 3.95, 110.0
+
+
+def build(g, T, topo, rank):
+    A = AluOpType
+    F = ActivationFunctionType
+    V, S, P, Q = g.vector, g.scalar, g.tensor, g.sync
+    cores = T.cores
+    n = len(cores)
+    me = cores[rank]
+    ops = []
+    lead = [0.0]
+    txn = {}
+    tag = [""]
+
+    def op(eng, fn, r, w, cost, lat=0.0, sem=None, cnt=0, after=None, bias=0.0, kind=""):
+        bank = None
+        for x in w:
+            if x[:2] in ("#x", "#w"):
+                if eng == "P":
+                    txn[x] = len(ops)
+                bank = (int(x[2]), txn[x])
+        ops.append({"bank": bank, "free": eng == "X", "e": eng, "fn": fn, "r": list(r), "w": list(w), "c": cost, "lat": lat,
+                    "sem": sem, "cnt": cnt, "after": after, "bias": bias + lead[0], "kind": kind, "tag": tag[0]})
+        return len(ops) - 1
+
+    def vc(nel, f=1.0):
+        return max(64.0, nel * f) * CY + 30
+
+    def ts(out, in0, s1, s2, o0, o1, r, w, nel, f=1.0):
+        if o1 is None:
+            return op("V", lambda: V.tensor_scalar(out, in0, s1, None, o0), r, w, vc(nel, f))
+        return op("V", lambda: V.tensor_scalar(out, in0, s1, s2, o0, o1), r, w, vc(nel, f))
+
+    def tt(out, a, b, o, r, w, nel, f=2.0):
+        return op("V", lambda: V.tensor_tensor(out, a, b, o), r, w, vc(nel, f))
+
+    def xs(out, in_, scale, bias, r, w, nel):
+        return op("X", (lambda: V.tensor_scalar(out, in_, scale, bias, A.mult, A.add),
+                        lambda: S.activation(out, in_, F.Identity, bias=bias, scale=scale)), r, w, vc(nel))
+
+    def cp(out, in_, r, w, nel, f=1.0):
+        return op("V", lambda: V.tensor_copy(out, in_), r, w, vc(nel, f))
+
+    def ms(ap, val, w, nel):
+        return op("V", lambda: V.memset(ap, val), [], w, vc(nel))
+
+    def scan(out, d0, d1, init, o0, o1, r, w, nel):
+        return op("V", lambda: V.tensor_tensor_scan(out, d0, d1, init, o0, o1), r, w, vc(nel))
+
+    def io(out, pat, base, cm, w, nel, isint=False):
+        if isint:
+            return op("G", lambda: g.iota(out, pat, base, cm), [], w, 130 + 2 * nel * CY)
+        return op("G", lambda: g.iota(out, pat, base, cm, allow_small_or_imprecise_dtypes=True), [], w, 130 + 2 * nel * CY)
+
+    def mm(lst, r, w):
+        def fn():
+            last = None
+            for (o, l, x, a, b, _c) in lst:
+                last = P.matmul(o, l, x, a, b)
+            return last
+        return op("P", fn, r, w, sum(x[5] for x in lst) * PC + 30)
+
+    ndma = [0]
+
+    def dma(pairs, r, w, nbytes, eng="Q", bias=0.0):
+        sem = "q%d" % ndma[0]
+        ndma[0] += 1
+        q = Q if eng == "Q" else S
+
+        def fn():
+            for (o, i) in pairs:
+                q.dma_start(o, i).then_inc(T.sem[sem], 16)
+        return op(eng, fn, r, w, 60.0 * len(pairs), lat=1800 + nbytes / 180.0, sem=sem, cnt=16 * len(pairs), bias=bias)
+
+    rloc = [0]
+
+    def remote(trs, r, nbytes, bias=0.0):
+        lst = []
+        for (src, dsts, lo, k, sem) in trs:
+            to = [cores[(rank + d) % n] for d, _x in dsts]
+            m = 0
+            for e in topo.engines(me, to[0])[lo:lo + k]:
+                m |= 1 << e
+            lst.append(RemoteDMATransfer(dst_ids=[DstId(rid=topo.addr(c)[0], pnc=topo.addr(c)[1]) for c in to], dma_engine_mask=m,
+                                         remote_sem=T.sem[sem], srcs=[src], dsts=[x for _d, x in dsts]))
+            rloc[0] += k
+        return op("G", lambda: g.remote_dma_fused(lst, local_sem=T.sem.rloc), r, [], 400.0, lat=2500 + nbytes / 120.0,
+                  sem="none", bias=bias)
+
+    def recv(sem, cnt, w, after):
+        return op("R", None, [], w, 0.0, sem=sem, cnt=cnt, after=after)
+
+    cc, oo = T.cc, T.oo
+    pcol, gcol, tcol, wcol, c12, nlc, p16, s1c, s2c, s3c = [cc[:, i:i + 1] for i in range(10)]
+    O = {}
+    for i, nm in enumerate(["mc", "lc", "nc", "x", "ko", "win", "a", "b", "dm", "m3", "j", "jo", "d1", "d2", "c", "b2"]):
+        O[nm] = oo[:, 12 * i:12 * i + 12]
+    PF = [T["pf%d" % i] for i in range(6)]
+    PX = [T.px0, T.px1]
+    WT = [T.w0, T.w1]
+    EE = [T.e0, T.e1]
+    GG = [T.g0, T.g1]
+    ne = len(topo.engines(me, cores[(rank + 1) % n]))
+
+    sl = slice(512 * rank, 512 * rank + 512)
+    dma([(T.tws[:, :], T.twist[:, sl])], [], ["tws"], 131072, bias=9000)
+    dma([(T.ti[0:8, :], T.turn[:, sl])], [], ["ti"], 16384, eng="S", bias=9000)
+    dma([(T.imgi[:, :], T.img[:, :])], [], ["imgi"], 98304, eng="S", bias=3000)
+    dma([(T.lfi[:, 256 * c:256 * c + 256], T.ent[:, W * c:W * c + W]) for c in range(3)] + [(T.lfi[:, 768:1024], T.elen[:, :])],
+        [], ["lfi"], 600000, bias=8000)
+    dma([(T.tw[:, :], T.twist[:, :])], [], ["tw"], 1400000)
+    io(T.owi[:, :], [[0, K]], 0, 0, ["owi"], K, True)
+    dma([(T.owi[4 * c::16, :], T.own[:, K * c:K * c + K]) for c in range(3)] + [(T.owi[12::16, :], T.olen[:, :])],
+        [], ["owi"], 30000)
+
+    lead[0] = 9000.0
+    io(T.ci[:, 0:1], [[0, 1]], 0, 1, ["ci0"], 1, True)
+    io(T.ig[:, :], [[16, 8], [0, 16]], 0, 0, ["ig"], 128)
+    io(T.it[:, :], [[0, 8], [1, 16]], 0, 0, ["it"], 128)
+    io(T.ia[:, :], [[1, 144]], -15, 0, ["ia"], 144)
+    lead[0] = 0.0
+    io(T.ik[:, :], [[16, 2], [32, 4]], 0, 0, ["ik"], 8)
+    io(T.i32[:, :], [[0, 8], [1, 32]], 0, 0, ["i32"], 256)
+    io(T.ij[:, :], [[16, 12]], 0, 0, ["ij"], 12)
+    lead[0] = 9000.0
+    ts(T.ci[:, 1:2], T.ci[:, 0:1], 112, None, A.bitwise_and, None, ["ci0"], ["ci1"], 1)
+    ts(T.ci[:, 2:3], T.ci[:, 0:1], 15, None, A.bitwise_and, None, ["ci0"], ["ci2"], 1)
+    cp(cc[:, 0:3], T.ci[:, 0:3], ["ci0", "ci1", "ci2"], ["c012"], 3)
+    ts(T.t1[:, :], T.it[:, :], 13.0, 0.5, A.is_lt, A.mult, ["it"], ["t1"], 128)
+    ts(T.t2[:, 0:128], T.it[:, :], 0.0, None, A.is_equal, None, ["it"], ["t2"], 128)
+    scan(T.pr[:, :], T.t1[:, :], T.t2[:, 0:128], 0.0, A.mult, A.add, ["t1", "t2"], ["pr"], 128)
+    ts(c12, tcol, -1.0, 12.0, A.mult, A.add, ["c012"], ["c12"], 1)
+    ts(T.t4[:, 0:16], T.it[:, 0:16], c12, 8.0, A.is_equal, A.mult, ["it", "c12"], ["t4a"], 16)
+    tt(T.t4[:, 32:48], T.t4[:, 0:16], T.pr[:, 0:16], A.mult, ["t4a", "pr"], ["t4c"], 16)
+    op("V", lambda: V.tensor_reduce(wcol, T.t4[:, 32:48], AxisListType.X, A.add), ["t4c"], ["wcol"], vc(16))
+    ts(T.t2[:, 128:256], T.ig[:, :], gcol, wcol, A.is_equal, A.mult, ["ig", "c012", "wcol"], ["t2b"], 128)
+    tt(T.ws[:, :], T.t2[:, 128:256], T.pr[:, :], A.mult, ["t2b", "pr"], ["ws"], 128)
+    ts(p16, pcol, 16.0, None, A.mult, None, ["c012"], ["p16"], 1)
+    ts(T.t3[0:8, :], T.ig[0:8, :], cc[0:8, 6:7], None, A.is_equal, None, ["ig", "p16"], ["t3"], 128)
+    tt(T.wt[0:8, :], T.t3[0:8, :], T.pr[0:8, :], A.mult, ["t3", "pr"], ["wt"], 128)
+    ts(T.eps[0:1, :], T.pr[0:1, :], 2.0 ** -10, None, A.mult, None, ["pr"], ["eps"], 128)
+    ms(T.one[0:1, :], 1.0, ["one"], 256)
+    ts(T.idb[:, :], T.ia[:, 15:143], pcol, None, A.is_equal, None, ["ia", "c012"], ["idb"], 128)
+    ts(T.n256[:, :], T.ia[:, 15:143], pcol, -256.0, A.is_equal, A.mult, ["ia", "c012"], ["n256"], 128)
+    lead[0] = 0.0
+    ts(T.ma[:, :], T.it[:, 0:16], tcol, None, A.is_equal, None, ["it", "c012"], ["ma"], 16)
+    ts(T.idh[:, :], T.ia[:, 15:143], pcol, None, A.is_equal, None, ["ia", "c012"], ["idh"], 128)
+    ts(nlc, tcol, 12.0, None, A.not_equal, None, ["c012"], ["nlc"], 1)
+    ts(T.ide[:, :], T.ia[:, 15:143], pcol, nlc, A.is_equal, A.mult, ["ia", "c012", "nlc"], ["ide"], 128)
+    ts(T.zo[:, :], T.ia[:, :], gcol, None, A.is_equal, None, ["ia", "c012"], ["zo"], 144)
+    ts(T.zl[:, :], T.ia[:, :], gcol, T.ma[:, 12:13], A.is_equal, A.mult, ["ia", "c012", "ma"], ["zl"], 144)
+    ts(T.zd[:, :], T.ia[:, :], gcol, wcol, A.is_equal, A.mult, ["ia", "c012", "wcol"], ["zd"], 144)
+    ts(T.bd[:, :], T.ig[:, :], gcol, None, A.is_equal, None, ["ig", "c012"], ["bd"], 128)
+    tt(s1c, T.ma[:, 4:5], T.ma[:, 0:1], A.subtract, ["ma"], ["s1c"], 1)
+    tt(s2c, T.ma[:, 8:9], T.ma[:, 4:5], A.subtract, ["ma"], ["s2c"], 1)
+    ts(s3c, T.ma[:, 8:9], -1.0, None, A.mult, None, ["ma"], ["s3c"], 1)
+    for q, (c, nm) in enumerate([(s1c, "s1c"), (s2c, "s2c"), (s3c, "s3c")]):
+        ts(T.sd[:, 128 * q:128 * q + 128], T.bd[:, :], c, None, A.mult, None, ["bd", nm], ["sd%d" % q], 128, 0.5)
+    ts(T.bdb[:, :], T.ig[:, :], gcol, None, A.is_equal, None, ["ig", "c012"], ["bdb"], 128)
+    ts(T.zob[:, :], T.ia[:, 3:131], gcol, None, A.is_equal, None, ["ia", "c012"], ["zob"], 128)
+    for a in range(16):
+        for (o_, i_, nm, ni) in ((T.bda, T.bdb, "bda", "bdb"), (T.bdl, T.zob, "bdl", "zob")):
+            op("S", lambda a=a, o_=o_, i_=i_: S.activation(o_[:, 128 * a:128 * a + 128], i_[:, :], F.Identity, scale=T.ma[:, a:a + 1]),
+               [ni, "ma"], [nm + "%d" % a], vc(128))
+    BDA = ["bda%d" % a for a in range(16)]
+    BDL = ["bdl%d" % a for a in range(16)]
+    ts(T.wk[:, :], T.ik[:, :], gcol, 16.0, A.is_equal, A.mult, ["ik", "c012"], ["wk"], 8)
+    ts(T.rs[:, :], T.i32[:, :], 0.0, -2.0 ** 20, A.is_equal, A.mult, ["i32"], ["rs"], 256)
+    ts(T.rm[0:1, 0:256], T.i32[0:1, :], 16.0, -65536.0, A.is_ge, A.mult, ["i32"], ["rm0"], 256)
+    ts(T.rm[0:1, 256:512], T.i32[0:1, :], -1.0, 15.0, A.mult, A.add, ["i32"], ["rm1"], 256)
+    tt(T.c15[0:1, :], T.rm[0:1, 0:256], T.rm[0:1, 256:512], A.add, ["rm0", "rm1"], ["c15"], 256)
+    ms(T.c49[0:1, :], 49152.0, ["c49"], 256)
+    ms(T.zz[:, :], 0.0, ["zz"], 97)
+    ms(T.ee[:, 192::194], 16384.0, ["eec"], 12)
+    ts(O["j"], T.ij[:, :], tcol, None, A.add, None, ["ij", "c012"], ["j"], 12)
+    ts(O["jo"], O["j"], 1.0 / 256, -0.75, A.mult, A.add, ["j"], ["jo"], 12)
+    ts(O["d1"], O["j"], 2048.0, None, A.add, None, ["j"], ["d1"], 12)
+    ts(O["d2"], O["j"], 4096.0, None, A.add, None, ["j"], ["d2"], 12)
+    io(T.w0[:, 0:536], [[0, 536]], 0, 0, ["w0f0"], 536)
+    for h in range(3):
+        k = 536 << h
+        op("S", lambda k=k: S.activation(T.w0[:, k:2 * k], T.w0[:, 0:k], F.Identity), ["w0f%d" % x for x in range(h + 1)],
+           ["w0f%d" % (h + 1)], vc(k))
+
+    lead[0] = 9000.0
+    ts(T.tc[0:8, :], T.ti[0:8, :], -1.0, 2048.0, A.mult, A.add, ["ti"], ["tc"], 512)
+    mm([(PX[0][:, :], T.eps[0:1, :], T.one[0:1, :], True, False, 512), (PX[0][:, :], T.ws[:, :], T.tws[:, :], False, False, 512),
+        (PX[0][:, :], T.wt[0:8, :], T.tc[0:8, :], False, True, 512)], ["ws", "tws", "wt", "tc", "eps", "one"], ["#x0"])
+    ts(T.zr[:, :], PX[0][:, :], 1.5 * 2 ** 23, 1.5 * 2 ** 23, A.add, A.subtract, [], ["#x0", "zr"], 512)
+    tt(T.zb[:, :], T.zr[:, :], PX[0][:, :], A.is_gt, ["zr"], ["#x0", "zb"], 512, 1.0)
+    mm([(PX[1][:, :], T.idb[:, :], T.tws[:, :], True, False, 512), (PX[1][:, :], T.n256[:, :], T.zb[:, :], False, True, 512)],
+       ["idb", "tws", "n256", "zb"], ["#x1"])
+    c0 = (512 * rank + 2048) % W
+    mine = T.wv[:, c0:c0 + 512]
+    op("S", lambda: S.activation(mine, PX[1][:, :], F.Identity), [], ["#x1", "wvm"], vc(512))
+    o = remote([(mine, [(d, mine) for d in range(1, n)], 0, ne, "rvw")], ["wvm"], 7 * 131072, bias=5000)
+    recv("rvw", ne * (n - 1), ["wvr"], o)
+    lead[0] = 0.0
+
+    cp(T.lf[:, :], T.lfi[:, :], ["lfi"], ["lf"], 1024)
+
+    def unfold(k, src, c0, r):
+        return dma([(WT[k % 2][4 * c::16, 0:W], src[:, c0 + 256 * c:c0 + 256 * c + 256]) for c in range(4)], r, ["w%d" % (k % 2)], 700000)
+
+    def send_table(k, extra):
+        o = remote([(T.lf[:, :], [(k, T.tl[:, 1024 * (k - 1):1024 * k])], 0, ne, "rt%d" % k)], ["lf"] + extra, 524288)
+        recv("rt%d" % k, ne, ["tl%d" % k], o)
+
+    unfold(0, T.lf, 0, ["lf", "w0f0", "w0f1", "w0f2", "w0f3"])
+    send_table(1, ["wvr"])
+    for h in range(4):
+        i = io(T.w1[:, 1072 * h:1072 * h + 1072], [[0, 1072]], 0, 0, ["w1"], 1072)
+        ops[i]["after"] = o
+    unfold(1, T.tl, 0, ["tl1"])
+    dma([(T.wv[:, W * c:W * c + W], T.wv[:, 0:W]) for c in range(1, 4)], ["wvm", "wvr"], ["wv1"], 3200000)
+
+    def scatter(s, d):
+        tag[0] = "s%d%d" % (s, d)
+        k = d + s - 1
+        i = DELTAS.index((s, d))
+        win = WT[k % 2]
+        op("V", lambda: V.tensor_copy(win[:, 0:TWW].indirect(T.dl[:, DLW * i + K:DLW * i + K + 12]), T.dl[:, DLW * i:DLW * i + K]),
+           ["dl%d%d" % (s, d)], ["w%d" % (k % 2)], 50 + K * SCC, kind="s")
+
+    ts(EE[0][:, :], T.owi[:, :], -2048.0, None, A.add, None, ["owi"], ["e0_0", "e0_1"], K)
+    mm([(PX[1][:, 0:12], T.zl[:, 15 - a:143 - a], EE[0][:, a::16], a == 0, a == 15, 64) for a in range(16)],
+       ["zl", "e0_0", "e0_1"], ["#w14"])
+    cp(O["mc"], PX[1][:, 0:12], [], ["#w14", "mc"], 12)
+    cp(T.uu[:, :], T.imgi[:, :], ["imgi"], ["u0", "u1"], K)
+    ts(T.bc[:, :], T.imgi[:, :], -2048.0, None, A.add, None, ["imgi"], ["bc0", "bc1"], K)
+
+    def gather(b, win, wr, out, nm):
+        for l0 in range(LB * b, LB * b + LB, GL):
+            o_, i_ = out[:, 16 * l0:16 * (l0 + GL)], win.indirect(T.uu[:, l0:l0 + GL])
+            op("X", (lambda o_=o_, i_=i_: V.tensor_copy(o_, i_), lambda o_=o_, i_=i_: S.activation(o_, i_, F.Identity)),
+               wr + ["u%d" % b], [nm + "_%d" % (l0 // GL)], 60 + 16 * GL * GC, kind="g")
+
+    def pieces(nm, l0, l1):
+        return [nm + "_%d" % k for k in range(l0 // GL, (l1 + GL - 1) // GL)]
+
+    for b in range(NB):
+        gather(b, T.tw[:, 0:W], ["tw"], T.ff, "f0")
+
+    def to_list(b, add, plain):
+        ls = slice(LB * b, LB * b + LB)
+        x = "#x%d" % b
+        u = ["u%d" % b]
+        if plain:
+            ts(T.uu[:, ls], PX[b][:, 0:LB], add, None, A.add, None, [], [x] + u, LB)
+        else:
+            ts(T.yi[:, ls], PX[b][:, 0:LB], add, None, A.add, None, [], [x, "yi%d" % b], LB)
+            ts(T.ya[:, ls], T.yi[:, ls], W - 1, None, A.bitwise_and, None, ["yi%d" % b], ["ya%d" % b], LB)
+            cp(T.uu[:, ls], T.ya[:, ls], ["ya%d" % b], u, LB)
+
+    def choose(s, b):
+        tag[0] = "c%d%d" % (s, b)
+        ls = slice(LB * b, LB * b + LB)
+        x = "#x%d" % b
+        X = PX[b]
+        c0 = 16 * LB * b
+        fr = ["ff%d" % ch for ch in range(3 * b, 3 * b + 3)] + pieces("f0", LB * b, LB * b + LB)
+        mm([(X[0:LB, 0:256], T.one[0:1, 0:LB], T.c15[0:1, :], True, False, 256)]
+           + [(X[0:LB, i:256:32], T.ff[:, c0 + i:c0 + 16 * LB:16], T.wk[:, :], False, i == 15, 64) for i in range(16)],
+           ["one", "c15", "wk"] + fr, [x])
+        scan(T.rm[0:LB, 256 * b:256 * b + 256], T.rs[0:LB, :], X[0:LB, 0:256], -2.0 ** 20, A.add, A.max, ["rs"], [x, "rm%d" % b], 256)
+        tt(T.mk[0:LB, 256 * b:256 * b + 240], X[0:LB, 0:240], T.rm[0:LB, 256 * b + 16:256 * b + 256], A.is_equal,
+           ["rm%d" % b], [x, "mk%d" % b], 240, 1.0)
+        mm([(X[:, 0:LB], T.mk[0:LB, 256 * b:256 * b + 128], T.idb[0:LB, 0:LB], True, False, LB),
+            (X[:, 0:LB], T.mk[0:LB, 256 * b + 112:256 * b + 240], T.idb[0:LB, 0:LB], False, True, LB)], ["mk%d" % b, "idb"], [x])
+        tt(T.mb[:, ls], X[:, 0:LB], T.bc[:, ls], A.mult, ["bc%d" % b], [x, "mb%d" % b], LB, 1.0)
+        nc = LB // 16
+        mm([(X[:, 0:nc], T.zo[:, 15 - a:143 - a], T.mb[:, LB * b + a:LB * b + LB:16], a == 0, a == 15, 64) for a in range(16)]
+           + [(X[:, 128:128 + LB], T.bd[:, :], T.mb[:, ls], True, True, LB)], ["zo", "bd", "mb%d" % b], [x])
+        os_ = slice(nc * b, nc * b + nc)
+        ts(T.wo[:, os_], X[:, 0:nc], 2048.0, None, A.add, None, [], [x, "wo%d" % b], nc)
+        E = EE[s % 2]
+        win = WT[(s - 1) % 2]
+        op("V", lambda: V.tensor_scalar(E[:, ls], win[:, 0:TWW].indirect(T.wo[:, os_]), -2048.0, None, A.add),
+           ["wo%d" % b, "w%d" % ((s - 1) % 2)], ["e%d_%d" % (s % 2, b)], 50 + LB * GC, kind="g")
+        xs(T.wf[:, os_], X[:, 0:nc], 1.0, 0.0, [], [x, "wf%d" % b], nc)
+        xs(T.wr[:, ls], X[:, 128:128 + LB], 1.0, 0.0, [], [x, "wr%d" % b], LB)
+        xs(T.wn[:, os_], T.wf[:, os_], -16384.0, 0.0, ["wf%d" % b], ["wn%d" % b], nc)
+        mm([(X[:, 0:LB], T.idh[:, :], T.bc[:, ls], True, False, LB), (X[:, 0:LB], T.bda[:, 0:128], E[:, ls], False, True, LB)],
+           ["idh", "bc%d" % b, "bda0", "e%d_%d" % (s % 2, b)], [x])
+        to_list(b, 6144.0, 3 * (s - 1) >= PLAIN)
+
+    def winners(s):
+        tag[0] = "w%d" % s
+        E, Ep = EE[s % 2], EE[(s - 1) % 2]
+        X, xw = PX[BK[0]], "#w%d1" % BK[0]
+        mm([(X[:, 256:268], T.zl[:, 15 - a:143 - a], E[:, a::16], a == 0, a == 15, 64) for a in range(16)],
+           ["zl"] + ["e%d_%d" % (s % 2, b) for b in range(NB)], [xw])
+        xs(O["lc"], X[:, 256:268], 1.0, 0.0, [], [xw, "lc"], 12)
+        tt(O["nc"], O["mc"], O["lc"], A.is_ge, ["mc", "lc"], ["nc"], 12)
+        xs(O["x"], O["nc"], 8192.0, -2048.0, ["nc"], ["x"], 12)
+        tt(T.oh[:, 0:12], O["mc"], O["x"], A.max, ["mc", "x"], ["oh0"], 12)
+        ts(T.oh[:, 12:24], T.oh[:, 0:12], -1.0, None, A.mult, None, ["oh0"], ["oh1"], 12)
+        X, xw = PX[BK[1]], "#w%d2" % BK[1]
+        mm([(X[:, 0:193], T.idb[:, :], T.zz[:, 0:193], True, False, 193)]
+           + [(X[:, a:192:16], T.bda[:, 128 * a:128 * a + 128], T.oh[:, 12:24], False, False, 64) for a in range(16)]
+           + [(X[:, a + 1:193:16], T.bda[:, 128 * a:128 * a + 128], T.oh[:, 0:12], False, a == 15, 64) for a in range(16)],
+           ["idb", "zz", "oh0", "oh1"] + BDA, [xw])
+        xs(T.dd[:, 0:193], X[:, 0:193], 1.0, -1.0 / 256, [], [xw, "dd"], 193)
+        X, xw = PX[BK[2]], "#w%d3" % BK[2]
+        mm([(X[:, 256:448], T.ide[:, :], Ep[:, :], True, False, K)]
+           + [(X[:, 256 + a:448:16], T.bdl[:, 128 * a:128 * a + 128], T.oh[:, 0:12], False, a == 15, 64) for a in range(16)],
+           ["ide", "oh0"] + ["e%d_%d" % ((s - 1) % 2, b) for b in range(NB)] + BDL, [xw])
+        ts(T.sv[:, DLW * (s - 1):DLW * (s - 1) + K], X[:, 256:448], 2048.0, None, A.add, None, [], [xw, "sv%da" % s], K)
+        for c in range(12):
+            e_ = T.ee[:, 194 * c:194 * c + K]
+            op("X", (lambda c=c, e_=e_: V.tensor_scalar(e_, T.wr[:, :], T.wf[:, c:c + 1], 16384.0, A.not_equal, A.mult),
+                     lambda c=c, e_=e_: S.activation(e_, T.wr[:, :], F.Abs, bias=T.wn[:, c:c + 1], scale=16384.0)),
+               ["wr0", "wr1", "wf%d" % (c // 6), "wn%d" % (c // 6)], ["ee%d" % c], vc(K))
+        for c in range(12):
+            scan(T.sc[:, 194 * c:194 * c + 193], T.dd[:, 0:193], T.ee[:, 194 * c:194 * c + 193], 16384.0, A.add, A.min,
+                 ["dd", "ee%d" % c, "eec"], ["sc%d" % c], 193)
+        tt(O["ko"], O["mc"], O["jo"], A.add, ["mc", "jo"], ["ko"], 12)
+        tt(O["a"], T.wf[:, :], O["d1"], A.subtract, ["wf0", "wf1", "d1"], ["a"], 12)
+        tt(O["win"], T.sc[:, 192::194], O["ko"], A.is_equal, ["ko"] + ["sc%d" % c for c in range(12)], ["win"], 12)
+        tt(O["b"], O["a"], O["win"], A.mult, ["a", "win"], ["b"], 12)
+        tt(O["c"], O["b"], O["d2"], A.add, ["b", "d2"], ["c"], 12)
+        cp(T.sv[:, DLW * (s - 1) + K:DLW * (s - 1) + K + 12], O["c"], ["c"], ["sv%db" % s], 12)
+        ds = [d for (s2, d) in DELTAS if s2 == s]
+        k = ne // {1: 1, 2: 2, 3: 4, 4: 4}[len(ds)]
+        src = T.sv[:, DLW * (s - 1):DLW * s]
+        o = remote([(src, [(d, T.dl[:, DLW * DELTAS.index((s, d)):DLW * (DELTAS.index((s, d)) + 1)])], k * (d - 1), k, "rd%d%d" % (s, d))
+                    for d in ds], ["sv%da" % s, "sv%db" % s], 60000)
+        for d in ds:
+            recv("rd%d%d" % (s, d), k, ["dl%d%d" % (s, d)], o)
+        if s < ST:
+            tt(O["dm"], O["lc"], O["mc"], A.subtract, ["lc", "mc"], ["dm"], 12)
+            xs(O["m3"], O["mc"], 1.0, 3.0, ["mc"], ["m3"], 12)
+            tt(O["b2"], O["dm"], O["win"], A.mult, ["dm", "win"], ["b2"], 12)
+            tt(O["mc"], O["m3"], O["b2"], A.add, ["m3", "b2"], ["mc"], 12)
+
+    def letter(s, q, b):
+        tag[0] = "l%d%d%d" % (s, q, b)
+        ls = slice(LB * b, LB * b + LB)
+        G = GG[(3 * s + q) % 2]
+        gn = "g%d" % ((3 * s + q) % 2)
+        if 3 * (s - 1) + q < PLAIN:
+            gather(b, T.wv[:, 0:W], ["wvm", "wvr"], G, gn)
+        else:
+            gather(b, T.wv[:, 0:4 * W], ["wvm", "wvr", "wv1"], G, gn)
+        X = PX[b]
+        c0 = 16 * LB * b
+        mm([(X[:, 0:LB], T.sd[:, 128 * q:128 * q + 128], EE[s % 2][:, ls], True, False, LB)]
+           + [(X[:, 0:LB], T.zd[:, 15 - i:143 - i], G[:, c0 + i:c0 + 16 * LB:16], False, i == 15, LB) for i in range(16)],
+           ["sd%d" % q, "e%d_%d" % (s % 2, b), "zd"] + pieces(gn, LB * b, LB * b + LB), ["#x%d" % b])
+        for ch in range(3 * b, 3 * b + 3):
+            cs = slice(512 * ch, 512 * ch + 512)
+            if q == 0:
+                mm([(PF[ch][:, :], T.one[0:1, 0:128], T.c49[0:1, :], True, False, 512), (PF[ch][:, :], T.idb[:, :], T.ff[:, cs], False, False, 512)],
+                   ["one", "c49", "idb", "ff%d" % ch] + pieces("f0", 32 * ch, 32 * ch + 32), ["#f%d" % ch])
+            mm([(PF[ch][:, :], T.idb[:, :], G[:, cs], False, q == 2, 512)], ["idb"] + pieces(gn, 32 * ch, 32 * ch + 32), ["#f%d" % ch])
+        if q < 2:
+            to_list(b, 8192.0, 3 * (s - 1) + q + 1 >= PLAIN)
+            return
+        ts(T.yi[:, ls], X[:, 0:LB], 8192.0, None, A.add, None, [], ["#x%d" % b, "yi%d" % b], LB)
+        ts(T.ya[:, ls], T.yi[:, ls], W - 1, None, A.bitwise_and, None, ["yi%d" % b], ["ya%d" % b], LB)
+        if s < ST:
+            ts(T.bc[:, ls], T.ya[:, ls], -2048.0, None, A.add, None, ["ya%d" % b], ["bc%d" % b], LB)
+        else:
+            cp(T.yo[:, ls], T.ya[:, ls], ["ya%d" % b], ["yo%d" % b], LB)
+            dma([(T.yimg[:, ls], T.yo[:, ls])], ["yo%d" % b], [], 50000)
+        for ch in range(3 * b, 3 * b + 3):
+            cs = slice(512 * ch, 512 * ch + 512)
+            xs(T.kk[:, cs], PF[ch][:, :], 1.0, -127.5, [], ["#f%d" % ch, "kk%d" % ch], 512)
+            tt(T.ff[:, cs], PF[ch][:, :], T.kk[:, cs], A.subtract, ["kk%d" % ch], ["#f%d" % ch, "ff%d" % ch, "f0_%d" % ch], 512, 1.0)
+            if s == ST:
+                dma([(T.yf[:, cs], T.ff[:, cs])], ["ff%d" % ch], [], 131072)
+
+    for s in range(1, ST + 1):
+        if s > 1:
+            scatter(s - 1, 1)
+        for b in range(NB):
+            choose(s, b)
+        if s < ST:
+            if s == 1:
+                for k in range(2, 5):
+                    send_table(k, ["e1_0", "tl1"])
+            unfold(s + 1, T.tl, 1024 * s, ["tl%d" % (s + 1)])
+            for s2 in range(1, s):
+                scatter(s2, s + 2 - s2)
+        winners(s)
+        if s < ST:
+            scatter(s, 2)
+        for q in range(3):
+            for b in range(NB):
+                letter(s, q, b)
+    scatter(ST, 1)
+    dma([(T.yent[:, W * c:W * c + W], T.w0[4 * c::16, 0:W]) for c in range(3)] + [(T.yelen[:, :], T.w0[12::16, 0:W])], ["w0"], [], 600000)
+    ops[3]["after"] = 0
+    ops[4]["after"] = 3
+    return ops, rloc[0]
+
+
+def plan(ops):
+    nops = len(ops)
+    state = [SEED * 7919 + 1]
+
+    def rnd():
+        state[0] = (state[0] * 1103515245 + 12345) % 2147483648
+        return state[0] / 2147483648.0
+    lean = {}
+    for o in ops:
+        if o["tag"] not in lean:
+            lean[o["tag"]] = JT * (rnd() - 0.5)
+    lastw, readers = {}, {}
+    pred = [dict() for _ in ops]
+    for i, o in enumerate(ops):
+        if o["after"] is not None:
+            pred[i][o["after"]] = 0
+        for w in o["w"]:
+            for j in readers.get(w, []) + ([lastw[w]] if w in lastw else []):
+                pred[i][j] = max(pred[i].get(j, 0), 1 if w[0] == "#" else 2)
+        for r in o["r"]:
+            if r in lastw:
+                pred[i][lastw[r]] = 2
+        for r in o["r"]:
+            readers.setdefault(r, []).append(i)
+        for w in o["w"]:
+            lastw[w] = i
+            readers[w] = []
+
+    def hard(i, j, e):
+        k = pred[i][j]
+        return k == 2 or (k == 1 and ops[j]["e"] != e)
+
+    def gap(i, j, e):
+        if pred[i][j] == 0 and ops[i]["e"] == ops[j]["e"]:
+            return -ops[j]["lat"]
+        return LAT if hard(i, j, e) else 0.0
+    succ = [[] for _ in ops]
+    for i in range(nops):
+        for j in pred[i]:
+            succ[j].append(i)
+    prio = [0.0] * nops
+    for i in range(nops - 1, -1, -1):
+        prio[i] = ops[i]["c"] + ops[i]["lat"] + LAT + max([prio[k] for k in succ[i]] + [0.0])
+    for i in range(nops):
+        prio[i] += ops[i]["bias"] + JG * rnd() + lean[ops[i]["tag"]]
+    left = [len(pred[i]) for i in range(nops)]
+    ready = [i for i in range(nops) if left[i] == 0]
+    done = [0.0] * nops
+    free, base, size = {}, {}, {}
+    for o in ops:
+        size[o["bank"]] = size.get(o["bank"], 0) + 1
+    held = {0: None, 1: None}
+    users = {0: [], 1: []}
+    while ready:
+        cand = []
+        for i in ready:
+            bk = ops[i]["bank"]
+            if bk is not None and held[bk[0]] not in (None, bk):
+                continue
+            for e in ("VS" if ops[i]["e"] == "X" else ops[i]["e"]):
+                if (i, e) not in base:
+                    base[(i, e)] = max([done[j] + gap(i, j, e) for j in pred[i]] + [0.0])
+                t = base[(i, e)] if e == "R" else max(base[(i, e)], free.get(e, 0.0))
+                if bk is not None and bk[1] == i:
+                    t = max([t] + [done[j] + LAT for j in users[bk[0]] if ops[j]["e"] != e])
+                cand.append((t + (VPEN if ops[i]["e"] == "X" and e == "V" else 0.0), -prio[i], i, e, t))
+        best = min(cand)
+        e = best[3]
+        if e != "R":
+            best = min([c for c in cand if c[3] == e and c[0] <= best[0] + WIN], key=lambda c: c[1])
+        i, t = best[2], best[4]
+        ops[i]["e"] = e
+        ready.remove(i)
+        bk = ops[i]["bank"]
+        if bk is not None:
+            if bk[1] == i:
+                for j in users[bk[0]]:
+                    pred[i][j] = max(pred[i].get(j, 0), 1)
+                users[bk[0]] = []
+            users[bk[0]].append(i)
+            size[bk] -= 1
+            held[bk[0]] = bk if size[bk] else None
+        if e != "R":
+            free[e] = t + ops[i]["c"]
+        done[i] = t + ops[i]["c"] + ops[i]["lat"]
+        for k in succ[i]:
+            left[k] -= 1
+            if left[k] == 0:
+                ready.append(k)
+    for i in range(nops):
+        succ[i] = []
+    for i in range(nops):
+        for j in pred[i]:
+            succ[j].append(i)
+
+    def place(key, back):
+        before, after = (succ, pred) if back else (pred, succ)
+        cnt = [len(before[i]) for i in range(nops)]
+        rdy = [i for i in range(nops) if cnt[i] == 0]
+        busy = {e: [] for e in "VSPGQ"}
+        st, en = [0.0] * nops, [0.0] * nops
+        while rdy:
+            i = min(rdy, key=lambda k: key[k])
+            rdy.remove(i)
+            o = ops[i]
+            best = None
+            for e in ("SV" if o["free"] else o["e"]):
+                o["e"] = e
+                t = max([en[j] + (gap(j, i, ops[j]["e"]) if back else gap(i, j, e)) for j in before[i]] + [0.0])
+                if back:
+                    t += o["lat"]
+                pos = 0
+                if e != "R":
+                    b = busy[e]
+                    pos = len(b)
+                    while pos > 0 and b[pos - 1][1] > t:
+                        pos -= 1
+                    while pos < len(b) and t + o["c"] > b[pos][0]:
+                        t = max(t, b[pos][1])
+                        pos += 1
+                if best is None or t + VPEN < best[0]:
+                    best = (t, e, pos)
+            t, e, pos = best
+            o["e"] = e
+            if e != "R":
+                busy[e].insert(pos, (t, t + o["c"]))
+            st[i] = t
+            en[i] = t + o["c"] + (0.0 if back else o["lat"])
+            for k in after[i]:
+                cnt[k] -= 1
+                if cnt[k] == 0:
+                    rdy.append(k)
+        return st, en
+
+    def score(order):
+        tot = 0.0
+        for gf, sf, pf, df, lf in ((1, 1, 1, 1, 1), (0.67, 0.5, 1, 0.7, 1), (1.33, 1.5, 1, 1, 1), (1, 1, 1, 0.6, 2), (1, 1, 0.8, 0.6, 0.5)):
+            dn, fr = [0.0] * nops, {}
+            for i in order:
+                o = ops[i]
+                t = fr.get(o["e"], 0.0) if o["e"] != "R" else 0.0
+                for j in pred[i]:
+                    x = gap(i, j, o["e"])
+                    if x >= 0:
+                        t = max(t, dn[j] + x * lf)
+                c = o["c"] * (gf if o["kind"] == "g" else sf if o["kind"] == "s" else pf if o["e"] == "P" else 1.0)
+                fr[o["e"]] = t + c
+                dn[i] = t + c + o["lat"] * df
+            tot += max(dn)
+        return tot
+
+    keep = None
+    for _it in range(ROUNDS):
+        st, en = place([-d for d in done], True)
+        start, done = place([-x for x in en], False)
+        order = sorted(range(nops), key=lambda i: (start[i], i))
+        sc = score(order)
+        if keep is None or sc < keep[0]:
+            keep = (sc, order, [{j: hard(i, j, ops[i]["e"]) for j in pred[i]} for i in range(nops)], start, done, [o["e"] for o in ops])
+    for i in range(nops):
+        ops[i]["e"] = keep[5][i]
+    return keep[1:5]
+
+
+def rank_program(g, core, T, topo):
+    rank = T.rank_of(core)
+    if rank is None:
+        return
+    ops, nloc = build(g, T, topo, rank)
+    order, pred, start, done = plan(ops)
+    queues = {"V": g.vector, "S": g.scalar, "P": g.tensor, "Q": g.sync, "G": g}
+    need = set()
+    for i in range(len(ops)):
+        for j, hard in pred[i].items():
+            if hard and ops[j]["sem"] is None:
+                need.add(j)
+    count = {e: 0 for e in queues}
+    mark = {}
+    seen = {e: {} for e in queues}
+    for i in order:
+        o = ops[i]
+        e = o["e"]
+        if e == "R":
+            continue
+        waits = {}
+        for j, hard in pred[i].items():
+            if not hard:
+                continue
+            if ops[j]["sem"] is None:
+                nm, c = "s" + ops[j]["e"], mark[j]
+            else:
+                nm, c = ops[j]["sem"], ops[j]["cnt"]
+            waits[nm] = max(waits.get(nm, 0), c)
+        for nm, c in waits.items():
+            if seen[e].get(nm, 0) < c:
+                queues[e].wait_ge(T.sem[nm], c)
+                seen[e][nm] = c
+        ins = o["fn"][0 if e == "V" else 1]() if o["free"] else o["fn"]()
+        if i in need:
+            count[e] += 1
+            mark[i] = count[e]
+            ins.then_inc(T.sem["s" + e], 1)
+    for o in ops:
+        if o["sem"] not in (None, "none") and max(seen[e].get(o["sem"], 0) for e in seen) < o["cnt"]:
+            g.sync.wait_ge(T.sem[o["sem"]], o["cnt"])
+    for e in "VSPG":
+        if count[e] and max(seen[x].get("s" + e, 0) for x in seen) < count[e]:
+            g.sync.wait_ge(T.sem["s" + e], count[e])
+    g.wait_ge(T.sem.rloc, nloc)

@@ -4,12 +4,19 @@ from concourse.mybir import AluOpType, AxisListType, ActivationFunctionType
 W, K, ST = 4096, 192, 4
 NB = 2
 LB = K // NB
-GL = 32
 TWW = W + K
 DLW = 204
-PLAIN = 4
 BK = (0, 1, 0)
-ROUNDS, VPEN, WIN, SEED, JG, JT = 8, 300.0, 100.0, 1079, 500.0, 3000.0
+PAR = dict(CUT=((48, 48), (48, 48), (32, 32, 32), (48, 48)),
+           PLAIN=3,
+           CHAIN=(2, 3, 4),
+           SPLIT=((0, 0), (1, 1)),
+           WHO={},
+           TOL=300.0, VP0=30.0, WB=2000.0, WIN2=0.0, WINF=0.4, SMALL=300.0, HALF=(1, 3), KS=(0, 1, 2, 3, 4, 5), WAV=12, WAB=8000.0,
+           ORDER=((0, 0), (0, 1), (1, 0), (0, 2), (1, 1), (1, 2)),
+           ROUNDS=2000, VPEN=400.0, WIN=30.0, SEED=1, JG=1500.0, JT=2000.0,
+           VARY=((1, 1, 1, 1, 1), (0.9, 0.7, 0.5, 1.2, 1), (1.25, 1.3, 1.4, 1, 1), (1, 0.7, 1.3, 1, 2.2), (1, 1.2, 1, 1.7, 1)),
+           CY=0.87, PC=0.435, GC=1.56, SCC=3.8, LAT=110.0, FIX=35.0, DL=1200.0, RL=1500.0, BW=330.0)
 DELTAS = [(s, d) for s in range(1, ST + 1) for d in range(1, ST + 2 - s)]
 
 
@@ -18,52 +25,53 @@ def sb(n, dtype):
 
 
 SCRATCH = {}
-for _n, _c in dict(tw=W, tws=512, wv=4 * W, g0=16 * K, g1=16 * K, ff=16 * K, kk=16 * K, zb=512, mk=512, ee=12 * 194, zd=144, idb=128,
-                   n256=128, bda=2048, bdl=2048, bdb=128, zob=128, wk=8, ws=128, c15=256, one=512, eps=128, zz=194, c49=512).items():
+for _n, _c in dict(tw=W, tws=512, wv=4 * W, g0=16 * K, g1=16 * K, g2=16 * K, ff=16 * K, kk=16 * K, zb=512, mk=512, ee=12 * 194, zd=144, idb=128,
+                   n256=128, bda=2048, bdb=128, wk=16, ws=128, c15=256, one=512, eps=128, c3=ST, c49=512,
+                   zo=144, zl=144, bdl=256, idn=128, ide=128, idl=128, sd=384).items():
     SCRATCH[_n] = sb(_c, "bfloat16")
-for _n, _c in dict(w0=TWW, w1=TWW, lf=1024, tl=4096, yo=K, zr=512, rm=512, wf=12, wr=K, wn=12, sc=12 * 194, dd=194, oo=16 * 12, cc=16,
-                   ia=144, ig=128, it=128, ik=8, i32=256, ij=12, ma=16, t1=128, t2=256, t3=128, pr=128, t4=64, rs=256).items():
+for _n, _c in dict(wb=TWW, wc=TWW, lf=1024, tf=1024, tl=4096, yo=K, zr=512, rm=512, wf=12, sc=12 * 194, dd=194, oo=16 * 12, cc=32,
+                   ia=144, ig=128, it=128, ik=8, ij=12, ma=16, t1=128, t2=256, t3=128, t5=128, t6=144, pr=128, t4=64, rs=256).items():
     SCRATCH[_n] = sb(_c, "float32")
-for _n, _c in dict(lfi=1024, imgi=K, yi=K, ya=K, owi=K, ti=512, ci=4).items():
+for _n, _c in dict(wa=W, lfi=1024, imgi=K, yi=K, ya=K, owi=K, ti=512, ci=4).items():
     SCRATCH[_n] = sb(_c, "int32")
 for _n, _c in dict(dl=DLW * len(DELTAS), sv=DLW * ST, uu=K, wo=12).items():
     SCRATCH[_n] = sb(_c, "uint16")
-for _n, _c in dict(bc=K, mb=K, e0=K, e1=K, tc=512, oh=24, zo=144, zl=144, idh=128, ide=128, bd=128, sd=384, wt=128).items():
+for _n, _c in dict(bc=K, mb=K, e0=K, e1=K, tc=512, th=16 * K, mc=12, wr=K, kr=194, wt=128).items():
     SCRATCH[_n] = sb(_c, "float16")
 for _n in ["pf%d" % _i for _i in range(6)] + ["px0", "px1"]:
     SCRATCH[_n] = ("psum", [128, 512], "float32")
 
-SEMAPHORES = (["sV", "sS", "sP", "sG", "rloc", "rvw"] + ["rt%d" % k for k in range(1, 5)]
-              + ["rd%d%d" % sd for sd in DELTAS] + ["q%d" % i for i in range(32)])
-
-CY, PC, GC, SCC, LAT = 1.04, 0.52, 1.62, 3.95, 110.0
+SEMAPHORES = (["sV", "sS", "sP", "sG", "rloc", "rvw"] + ["rt%d" % k for k in range(1, 5)] + ["rf%d" % k for k in range(1, 5)]
+              + ["rd%d%d" % sd for sd in DELTAS] + ["q%d" % i for i in range(36)])
 
 
 def build(g, T, topo, rank):
     A = AluOpType
     F = ActivationFunctionType
     V, S, P, Q = g.vector, g.scalar, g.tensor, g.sync
+    PLAIN, CHAIN, CY, PC, GC, SCC = [PAR[x] for x in ("PLAIN", "CHAIN", "CY", "PC", "GC", "SCC")]
     cores = T.cores
     n = len(cores)
     me = cores[rank]
     ops = []
     lead = [0.0]
-    txn = {}
     tag = [""]
+    gathers = {}
+    lists = [(s, d) for (s, d) in DELTAS if d == 1 or all(k not in CHAIN for k in range(s + 1, s + d))]
 
-    def op(eng, fn, r, w, cost, lat=0.0, sem=None, cnt=0, after=None, bias=0.0, kind=""):
+    def op(eng, fn, r, w, cost, lat=0.0, sem=None, cnt=0, after=None, bias=0.0, kind="", nbytes=0, more=0.0):
         bank = None
+        if eng == "Y":
+            eng, fn = "V", fn[0]
         for x in w:
             if x[:2] in ("#x", "#w"):
-                if eng == "P":
-                    txn[x] = len(ops)
-                bank = (int(x[2]), txn[x])
-        ops.append({"bank": bank, "free": eng == "X", "e": eng, "fn": fn, "r": list(r), "w": list(w), "c": cost, "lat": lat,
-                    "sem": sem, "cnt": cnt, "after": after, "bias": bias + lead[0], "kind": kind, "tag": tag[0]})
+                bank = int(x[2])
+        ops.append({"bank": bank, "free": eng == "X", "e": eng, "fn": fn, "r": list(r), "w": list(w), "c": cost, "lat": lat, "sem": sem,
+                    "cnt": cnt, "after": after, "behind": None, "more": more, "bytes": nbytes, "bias": bias + lead[0], "kind": kind, "tag": tag[0]})
         return len(ops) - 1
 
     def vc(nel, f=1.0):
-        return max(64.0, nel * f) * CY + 30
+        return max(64.0, nel * f) * CY + PAR["FIX"]
 
     def ts(out, in0, s1, s2, o0, o1, r, w, nel, f=1.0):
         if o1 is None:
@@ -73,9 +81,13 @@ def build(g, T, topo, rank):
     def tt(out, a, b, o, r, w, nel, f=2.0):
         return op("V", lambda: V.tensor_tensor(out, a, b, o), r, w, vc(nel, f))
 
-    def xs(out, in_, scale, bias, r, w, nel):
+    def xs(out, in_, scale, bias, r, w, nel, f=1.0, kind=""):
         return op("X", (lambda: V.tensor_scalar(out, in_, scale, bias, A.mult, A.add),
-                        lambda: S.activation(out, in_, F.Identity, bias=bias, scale=scale)), r, w, vc(nel))
+                        lambda: S.activation(out, in_, F.Identity, bias=bias, scale=scale)), r, w, vc(nel, f), more=vc(nel, max(f, 1.0)) - vc(nel, f),
+                  kind=kind)
+
+    def act(out, in_, scale, bias, r, w, nel, func=F.Identity):
+        return op("S", lambda: S.activation(out, in_, func, bias=bias, scale=scale), r, w, vc(nel))
 
     def cp(out, in_, r, w, nel, f=1.0):
         return op("V", lambda: V.tensor_copy(out, in_), r, w, vc(nel, f))
@@ -97,11 +109,11 @@ def build(g, T, topo, rank):
             for (o, l, x, a, b, _c) in lst:
                 last = P.matmul(o, l, x, a, b)
             return last
-        return op("P", fn, r, w, sum(x[5] for x in lst) * PC + 30)
+        return op("P", fn, r, w, sum(x[5] for x in lst) * PC)
 
     ndma = [0]
 
-    def dma(pairs, r, w, nbytes, eng="Q", bias=0.0):
+    def dma(pairs, r, w, nbytes, eng="Q", bias=0.0, after=None):
         sem = "q%d" % ndma[0]
         ndma[0] += 1
         q = Q if eng == "Q" else S
@@ -109,11 +121,12 @@ def build(g, T, topo, rank):
         def fn():
             for (o, i) in pairs:
                 q.dma_start(o, i).then_inc(T.sem[sem], 16)
-        return op(eng, fn, r, w, 60.0 * len(pairs), lat=1800 + nbytes / 180.0, sem=sem, cnt=16 * len(pairs), bias=bias)
+        return op(eng, fn, r, w, 60.0 * len(pairs), lat=PAR["DL"], nbytes=nbytes, sem=sem, cnt=16 * len(pairs), bias=bias, after=after)
 
     rloc = [0]
+    first = [True]
 
-    def remote(trs, r, nbytes, bias=0.0):
+    def remote(trs, r, nbytes, bias=0.0, local="rloc"):
         lst = []
         for (src, dsts, lo, k, sem) in trs:
             to = [cores[(rank + d) % n] for d, _x in dsts]
@@ -122,9 +135,13 @@ def build(g, T, topo, rank):
                 m |= 1 << e
             lst.append(RemoteDMATransfer(dst_ids=[DstId(rid=topo.addr(c)[0], pnc=topo.addr(c)[1]) for c in to], dma_engine_mask=m,
                                          remote_sem=T.sem[sem], srcs=[src], dsts=[x for _d, x in dsts]))
-            rloc[0] += k
-        return op("G", lambda: g.remote_dma_fused(lst, local_sem=T.sem.rloc), r, [], 400.0, lat=2500 + nbytes / 120.0,
-                  sem="none", bias=bias)
+            if local == "rloc":
+                rloc[0] += k
+        if first[0]:
+            first[0] = False
+            op("G", lambda: None, r, ["late"], 1700.0, sem="none", bias=bias)
+            r = r + ["late"]
+        return op("G", lambda: g.remote_dma_fused(lst, local_sem=T.sem[local]), r, [], 300.0, lat=PAR["RL"], nbytes=nbytes * 1.3, sem="none", bias=bias)
 
     def recv(sem, cnt, w, after):
         return op("R", None, [], w, 0.0, sem=sem, cnt=cnt, after=after)
@@ -132,293 +149,368 @@ def build(g, T, topo, rank):
     cc, oo = T.cc, T.oo
     pcol, gcol, tcol, wcol, c12, nlc, p16, s1c, s2c, s3c = [cc[:, i:i + 1] for i in range(10)]
     O = {}
-    for i, nm in enumerate(["mc", "lc", "nc", "x", "ko", "win", "a", "b", "dm", "m3", "j", "jo", "d1", "d2", "c", "b2"]):
+    for i, nm in enumerate(["mc", "x", "ko", "win", "a", "b", "dm", "j", "jo", "d1", "d2", "c", "b2"]):
         O[nm] = oo[:, 12 * i:12 * i + 12]
     PF = [T["pf%d" % i] for i in range(6)]
     PX = [T.px0, T.px1]
-    WT = [T.w0, T.w1]
+    WN = ["wa", "wb", "wc", "wb", "wc"]
+    WT = [T[x] for x in WN]
     EE = [T.e0, T.e1]
-    GG = [T.g0, T.g1]
+    GG = [T.g0, T.g1, T.g2]
     ne = len(topo.engines(me, cores[(rank + 1) % n]))
 
     sl = slice(512 * rank, 512 * rank + 512)
-    dma([(T.tws[:, :], T.twist[:, sl])], [], ["tws"], 131072, bias=9000)
-    dma([(T.ti[0:8, :], T.turn[:, sl])], [], ["ti"], 16384, eng="S", bias=9000)
-    dma([(T.imgi[:, :], T.img[:, :])], [], ["imgi"], 98304, eng="S", bias=3000)
-    dma([(T.lfi[:, 256 * c:256 * c + 256], T.ent[:, W * c:W * c + W]) for c in range(3)] + [(T.lfi[:, 768:1024], T.elen[:, :])],
-        [], ["lfi"], 600000, bias=8000)
-    dma([(T.tw[:, :], T.twist[:, :])], [], ["tw"], 1400000)
-    io(T.owi[:, :], [[0, K]], 0, 0, ["owi"], K, True)
+    d0 = dma([(T.ti[0:8, :], T.turn[:, sl])], [], ["ti"], 16384, bias=9000)
+    d0 = dma([(T.tws[:, :], T.twist[:, sl])], [], ["tws"], 131072, bias=9000, after=d0)
+    d0 = dma([(T.imgi[:, :], T.img[:, :])], [], ["imgi"], 98304, bias=3000, after=d0)
+    d1 = dma([(T.tw[:, :], T.twist[:, :])], [], ["tw"], 1048576, bias=8000, after=d0)
+    lead[0] = PAR["WAB"]
+    nv = PAR["WAV"]
+    ms(T.rs[:, :], 0.0, ["rs"], 256)
+    for h in range(nv):
+        o_ = T.wa[:, 256 * h:256 * h + 256]
+        op("X", (lambda o_=o_: V.memset(o_, 0), lambda o_=o_: S.activation(o_, T.rs[:, :], F.Identity)), ["rs"], ["wa%d" % h], vc(256))
+    fill = io(T.wa[:, 256 * nv:W], [[0, W - 256 * nv]], 0, 0, ["wag"], W - 256 * nv, True)
+    d2 = dma([(T.wa[4 * c::16, :], T.ent[:, W * c:W * c + W]) for c in range(3)] + [(T.wa[12::16, :], T.elen[:, :])],
+             ["wa%d" % h for h in range(nv)] + ["wag"], ["wa"], 524288, after=d1)
+    lead[0] = 0.0
+    lead[0] = 30000.0
+    ms(T.owi[:, :], 0, ["owi"], K)
     dma([(T.owi[4 * c::16, :], T.own[:, K * c:K * c + K]) for c in range(3)] + [(T.owi[12::16, :], T.olen[:, :])],
-        [], ["owi"], 30000)
+        [], ["owi"], 30000, after=d1)
 
     lead[0] = 9000.0
     io(T.ci[:, 0:1], [[0, 1]], 0, 1, ["ci0"], 1, True)
     io(T.ig[:, :], [[16, 8], [0, 16]], 0, 0, ["ig"], 128)
     io(T.it[:, :], [[0, 8], [1, 16]], 0, 0, ["it"], 128)
-    io(T.ia[:, :], [[1, 144]], -15, 0, ["ia"], 144)
-    lead[0] = 0.0
-    io(T.ik[:, :], [[16, 2], [32, 4]], 0, 0, ["ik"], 8)
-    io(T.i32[:, :], [[0, 8], [1, 32]], 0, 0, ["i32"], 256)
-    io(T.ij[:, :], [[16, 12]], 0, 0, ["ij"], 12)
-    lead[0] = 9000.0
+    ops[fill]["after"] = io(T.ia[:, :], [[1, 144]], -15, 0, ["ia"], 144)
     ts(T.ci[:, 1:2], T.ci[:, 0:1], 112, None, A.bitwise_and, None, ["ci0"], ["ci1"], 1)
     ts(T.ci[:, 2:3], T.ci[:, 0:1], 15, None, A.bitwise_and, None, ["ci0"], ["ci2"], 1)
     cp(cc[:, 0:3], T.ci[:, 0:3], ["ci0", "ci1", "ci2"], ["c012"], 3)
     ts(T.t1[:, :], T.it[:, :], 13.0, 0.5, A.is_lt, A.mult, ["it"], ["t1"], 128)
     ts(T.t2[:, 0:128], T.it[:, :], 0.0, None, A.is_equal, None, ["it"], ["t2"], 128)
     scan(T.pr[:, :], T.t1[:, :], T.t2[:, 0:128], 0.0, A.mult, A.add, ["t1", "t2"], ["pr"], 128)
-    ts(c12, tcol, -1.0, 12.0, A.mult, A.add, ["c012"], ["c12"], 1)
+    act(c12, tcol, -1.0, 12.0, ["c012"], ["c12"], 1)
     ts(T.t4[:, 0:16], T.it[:, 0:16], c12, 8.0, A.is_equal, A.mult, ["it", "c12"], ["t4a"], 16)
     tt(T.t4[:, 32:48], T.t4[:, 0:16], T.pr[:, 0:16], A.mult, ["t4a", "pr"], ["t4c"], 16)
     op("V", lambda: V.tensor_reduce(wcol, T.t4[:, 32:48], AxisListType.X, A.add), ["t4c"], ["wcol"], vc(16))
-    ts(T.t2[:, 128:256], T.ig[:, :], gcol, wcol, A.is_equal, A.mult, ["ig", "c012", "wcol"], ["t2b"], 128)
-    tt(T.ws[:, :], T.t2[:, 128:256], T.pr[:, :], A.mult, ["t2b", "pr"], ["ws"], 128)
-    ts(p16, pcol, 16.0, None, A.mult, None, ["c012"], ["p16"], 1)
+    ts(T.bdb[:, :], T.ig[:, :], gcol, None, A.is_equal, None, ["ig", "c012"], ["bdb"], 128)
+    tt(T.t2[:, 128:256], T.bdb[:, :], T.pr[:, :], A.mult, ["bdb", "pr"], ["t2b"], 128)
+    act(T.ws[:, :], T.t2[:, 128:256], wcol, 0.0, ["t2b", "wcol"], ["ws"], 128)
+    act(p16, pcol, 16.0, 0.0, ["c012"], ["p16"], 1)
     ts(T.t3[0:8, :], T.ig[0:8, :], cc[0:8, 6:7], None, A.is_equal, None, ["ig", "p16"], ["t3"], 128)
     tt(T.wt[0:8, :], T.t3[0:8, :], T.pr[0:8, :], A.mult, ["t3", "pr"], ["wt"], 128)
-    ts(T.eps[0:1, :], T.pr[0:1, :], 2.0 ** -10, None, A.mult, None, ["pr"], ["eps"], 128)
-    ms(T.one[0:1, :], 1.0, ["one"], 256)
-    ts(T.idb[:, :], T.ia[:, 15:143], pcol, None, A.is_equal, None, ["ia", "c012"], ["idb"], 128)
-    ts(T.n256[:, :], T.ia[:, 15:143], pcol, -256.0, A.is_equal, A.mult, ["ia", "c012"], ["n256"], 128)
-    lead[0] = 0.0
+    act(T.eps[0:1, :], T.pr[0:1, :], 2.0 ** -10, 0.0, ["pr"], ["eps"], 128)
+    ms(T.one[0:2, :], 1.0, ["one"], 256)
+    act(T.t5[:, :], T.ia[:, 15:143], -1.0, pcol, ["ia", "c012"], ["t5"], 128, F.Abs)
+    act(T.idb[:, :], T.t5[:, :], -1.0, 1.0, ["t5"], ["idb"], 128, F.Relu)
+    act(T.n256[:, :], T.idb[:, :], -256.0, 0.0, ["idb"], ["n256"], 128)
+    ma = [T.ma[:, a:a + 1] for a in range(16)]
+    lead[0] = 20000.0
     ts(T.ma[:, :], T.it[:, 0:16], tcol, None, A.is_equal, None, ["it", "c012"], ["ma"], 16)
-    ts(T.idh[:, :], T.ia[:, 15:143], pcol, None, A.is_equal, None, ["ia", "c012"], ["idh"], 128)
-    ts(nlc, tcol, 12.0, None, A.not_equal, None, ["c012"], ["nlc"], 1)
-    ts(T.ide[:, :], T.ia[:, 15:143], pcol, nlc, A.is_equal, A.mult, ["ia", "c012", "nlc"], ["ide"], 128)
-    ts(T.zo[:, :], T.ia[:, :], gcol, None, A.is_equal, None, ["ia", "c012"], ["zo"], 144)
-    ts(T.zl[:, :], T.ia[:, :], gcol, T.ma[:, 12:13], A.is_equal, A.mult, ["ia", "c012", "ma"], ["zl"], 144)
-    ts(T.zd[:, :], T.ia[:, :], gcol, wcol, A.is_equal, A.mult, ["ia", "c012", "wcol"], ["zd"], 144)
-    ts(T.bd[:, :], T.ig[:, :], gcol, None, A.is_equal, None, ["ig", "c012"], ["bd"], 128)
-    tt(s1c, T.ma[:, 4:5], T.ma[:, 0:1], A.subtract, ["ma"], ["s1c"], 1)
-    tt(s2c, T.ma[:, 8:9], T.ma[:, 4:5], A.subtract, ["ma"], ["s2c"], 1)
-    ts(s3c, T.ma[:, 8:9], -1.0, None, A.mult, None, ["ma"], ["s3c"], 1)
-    for q, (c, nm) in enumerate([(s1c, "s1c"), (s2c, "s2c"), (s3c, "s3c")]):
-        ts(T.sd[:, 128 * q:128 * q + 128], T.bd[:, :], c, None, A.mult, None, ["bd", nm], ["sd%d" % q], 128, 0.5)
-    ts(T.bdb[:, :], T.ig[:, :], gcol, None, A.is_equal, None, ["ig", "c012"], ["bdb"], 128)
-    ts(T.zob[:, :], T.ia[:, 3:131], gcol, None, A.is_equal, None, ["ia", "c012"], ["zob"], 128)
+    lead[0] = 0.0
+    act(T.c15[0:1, 0:16], T.it[0:1, 0:16], -1.0, 15.0, ["it"], ["c15"], 16)
+    act(T.c15[0:1, 16:32], T.it[0:1, 0:16], 0.0, -65536.0, ["it"], ["c15"], 16)
+    for k in (32, 64, 128):
+        act(T.c15[0:1, k:2 * k], T.c15[0:1, 0:k], 1.0, 0.0, [], ["c15"], k)
+    act(T.ij[:, 0:8], T.ig[:, 0::16], 1.0, 0.0, ["ig"], ["ija"], 8)
+    act(T.ij[:, 8:12], T.ig[:, 0:64:16], 1.0, 128.0, ["ig"], ["ijb"], 4)
+    act(T.ik[:, 0:4], T.ig[:, 0::32], 1.0, 0.0, ["ig"], ["ika"], 4)
+    act(T.ik[:, 4:8], T.ig[:, 16::32], 1.0, 0.0, ["ig"], ["ikb"], 4)
+    act(nlc, ma[12], -1.0, 1.0, ["ma"], ["nlc"], 1)
+    act(T.ide[:, :], T.idb[:, :], nlc, 0.0, ["idb", "nlc"], ["ide"], 128)
+    act(T.idl[:, :], T.idb[:, :], ma[12], 0.0, ["idb", "ma"], ["idl"], 128)
+    act(T.t6[:, :], T.ia[:, :], -1.0, gcol, ["ia", "c012"], ["t6"], 144, F.Abs)
+    act(T.zo[:, :], T.t6[:, :], -1.0, 1.0, ["t6"], ["zo"], 144, F.Relu)
+    for s in range(1, ST + 1):
+        act(cc[:, 16 + s:17 + s], ma[12], 3.0 * (s - 1), 2048.0, ["ma"], ["svc%d" % s], 1)
+    act(T.c3[0:1, :], T.it[0:1, 0:ST], 3.0, 0.0, ["it"], ["c3"], ST)
+    act(T.zl[:, :], T.zo[:, :], ma[12], 0.0, ["zo", "ma"], ["zl"], 144)
+    act(T.bdl[:, 0:128], T.bdb[:, :], ma[12], 0.0, ["bdb", "ma"], ["bdl"], 128)
+    act(T.bdl[:, 128:256], T.bdl[:, 0:128], -1.0, 0.0, ["bdl"], ["bdn"], 128)
+    act(T.idn[:, :], T.idb[:, :], -1.0, 0.0, ["idb"], ["idn"], 128)
+    act(T.zd[:, :], T.zo[:, :], wcol, 0.0, ["zo", "wcol"], ["zd"], 144)
+    for q, (c, lo, hi) in enumerate([(s1c, ma[0], ma[4]), (s2c, ma[4], ma[8]), (s3c, ma[8], 0.0)]):
+        act(c, lo, -1.0, hi, ["ma"], ["sc%dc" % q], 1)
+        act(T.sd[:, 128 * q:128 * q + 128], T.bdb[:, :], c, 0.0, ["bdb", "sc%dc" % q], ["sd%d" % q], 128)
     for a in range(16):
-        for (o_, i_, nm, ni) in ((T.bda, T.bdb, "bda", "bdb"), (T.bdl, T.zob, "bdl", "zob")):
-            op("S", lambda a=a, o_=o_, i_=i_: S.activation(o_[:, 128 * a:128 * a + 128], i_[:, :], F.Identity, scale=T.ma[:, a:a + 1]),
-               [ni, "ma"], [nm + "%d" % a], vc(128))
+        act(T.bda[:, 128 * a:128 * a + 128], T.bdb[:, :], ma[a], 0.0, ["bdb", "ma"], ["bda%d" % a], 128)
     BDA = ["bda%d" % a for a in range(16)]
-    BDL = ["bdl%d" % a for a in range(16)]
-    ts(T.wk[:, :], T.ik[:, :], gcol, 16.0, A.is_equal, A.mult, ["ik", "c012"], ["wk"], 8)
-    ts(T.rs[:, :], T.i32[:, :], 0.0, -2.0 ** 20, A.is_equal, A.mult, ["i32"], ["rs"], 256)
-    ts(T.rm[0:1, 0:256], T.i32[0:1, :], 16.0, -65536.0, A.is_ge, A.mult, ["i32"], ["rm0"], 256)
-    ts(T.rm[0:1, 256:512], T.i32[0:1, :], -1.0, 15.0, A.mult, A.add, ["i32"], ["rm1"], 256)
-    tt(T.c15[0:1, :], T.rm[0:1, 0:256], T.rm[0:1, 256:512], A.add, ["rm0", "rm1"], ["c15"], 256)
-    ms(T.c49[0:1, :], 49152.0, ["c49"], 256)
-    ms(T.zz[:, :], 0.0, ["zz"], 97)
-    ms(T.ee[:, 192::194], 16384.0, ["eec"], 12)
-    ts(O["j"], T.ij[:, :], tcol, None, A.add, None, ["ij", "c012"], ["j"], 12)
-    ts(O["jo"], O["j"], 1.0 / 256, -0.75, A.mult, A.add, ["j"], ["jo"], 12)
-    ts(O["d1"], O["j"], 2048.0, None, A.add, None, ["j"], ["d1"], 12)
-    ts(O["d2"], O["j"], 4096.0, None, A.add, None, ["j"], ["d2"], 12)
-    io(T.w0[:, 0:536], [[0, 536]], 0, 0, ["w0f0"], 536)
-    for h in range(3):
-        k = 536 << h
-        op("S", lambda k=k: S.activation(T.w0[:, k:2 * k], T.w0[:, 0:k], F.Identity), ["w0f%d" % x for x in range(h + 1)],
-           ["w0f%d" % (h + 1)], vc(k))
+    ts(T.wk[:, 0:8], T.ik[:, :], gcol, 16.0, A.is_equal, A.mult, ["ika", "ikb", "c012"], ["wk"], 8)
+    act(T.wk[:, 8:16], T.wk[:, 0:8], -1.0, 0.0, ["wk"], ["wkn"], 8)
+    ms(T.rs[:, 0::32], -2.0 ** 20, ["rs"], 8)
+    act(cc[0:2, 10:11], cc[0:2, 0:1], 127.5 - 49152.0, 49152.0, ["c012"], ["c49c"], 1)
+    act(T.c49[0:2, :], T.one[0:2, :], cc[0:2, 10:11], 0.0, ["one", "c49c"], ["c49"], 512)
+    ts(T.kr[:, 0:1], pcol, 0.0, None, A.mult, None, ["c012"], ["kr0"], 1)
+    ms(T.ee[:, 192::194], -193.0 / 256, ["eec"], 12)
+    act(O["j"], T.ij[:, :], 1.0, tcol, ["ija", "ijb", "c012"], ["j"], 12)
+    act(O["jo"], O["j"], 1.0 / 256, -0.75, ["j"], ["jo"], 12)
+    act(O["d1"], O["j"], 1.0, 2048.0, ["j"], ["d1"], 12)
+    act(O["d2"], O["j"], 1.0, 4096.0, ["j"], ["d2"], 12)
 
     lead[0] = 9000.0
-    ts(T.tc[0:8, :], T.ti[0:8, :], -1.0, 2048.0, A.mult, A.add, ["ti"], ["tc"], 512)
-    mm([(PX[0][:, :], T.eps[0:1, :], T.one[0:1, :], True, False, 512), (PX[0][:, :], T.ws[:, :], T.tws[:, :], False, False, 512),
-        (PX[0][:, :], T.wt[0:8, :], T.tc[0:8, :], False, True, 512)], ["ws", "tws", "wt", "tc", "eps", "one"], ["#x0"])
-    ts(T.zr[:, :], PX[0][:, :], 1.5 * 2 ** 23, 1.5 * 2 ** 23, A.add, A.subtract, [], ["#x0", "zr"], 512)
-    tt(T.zb[:, :], T.zr[:, :], PX[0][:, :], A.is_gt, ["zr"], ["#x0", "zb"], 512, 1.0)
-    mm([(PX[1][:, :], T.idb[:, :], T.tws[:, :], True, False, 512), (PX[1][:, :], T.n256[:, :], T.zb[:, :], False, True, 512)],
-       ["idb", "tws", "n256", "zb"], ["#x1"])
+    xs(T.tc[0:8, :], T.ti[0:8, :], -1.0, 2048.0, ["ti"], ["tc"], 512)
     c0 = (512 * rank + 2048) % W
     mine = T.wv[:, c0:c0 + 512]
-    op("S", lambda: S.activation(mine, PX[1][:, :], F.Identity), [], ["#x1", "wvm"], vc(512))
-    o = remote([(mine, [(d, mine) for d in range(1, n)], 0, ne, "rvw")], ["wvm"], 7 * 131072, bias=5000)
+    for h in range(2):
+        hs = slice(256 * h, 256 * h + 256)
+        Z, Y = PF[h][:, 0:256], PF[2 + h][:, 0:256]
+        mm([(Z, T.eps[0:1, :], T.one[0:1, hs], True, False, 256), (Z, T.ws[:, :], T.tws[:, hs], False, False, 256),
+            (Z, T.wt[0:8, :], T.tc[0:8, hs], False, True, 256)], ["ws", "tws", "wt", "tc", "eps", "one"], ["#f%d" % h])
+        ts(T.zr[:, hs], Z, 1.5 * 2 ** 23, 1.5 * 2 ** 23, A.add, A.subtract, [], ["#f%d" % h, "zr%d" % h], 256)
+        tt(T.zb[:, hs], T.zr[:, hs], Z, A.is_gt, ["zr%d" % h], ["#f%d" % h, "zb%d" % h], 256, 1.0)
+        mm([(Y, T.idb[:, :], T.tws[:, hs], True, False, 256), (Y, T.n256[:, :], T.zb[:, hs], False, True, 256)],
+           ["idb", "tws", "n256", "zb%d" % h], ["#f%d" % (2 + h)])
+        made = act(mine[:, hs], Y, 1.0, 0.0, [], ["#f%d" % (2 + h), "wvm%d" % h], 256)
+    o = remote([(mine, [(d, mine) for d in range(1, n)], 0, ne, "rvw")], ["wvm0", "wvm1"], 7 * 131072, bias=5000)
     recv("rvw", ne * (n - 1), ["wvr"], o)
     lead[0] = 0.0
 
-    cp(T.lf[:, :], T.lfi[:, :], ["lfi"], ["lf"], 1024)
+    dma([(T.lfi[:, 256 * c:256 * c + 256], T.ent[:, W * c:W * c + W]) for c in range(3)] + [(T.lfi[:, 768:1024], T.elen[:, :])],
+        ["wa"], ["lfi"], 524288)
+    for h in range(2):
+        xs(T.lf[:, 512 * h:512 * h + 512], T.lfi[:, 512 * h:512 * h + 512], 1.0, 0.0, ["lfi"], ["lf%d" % h], 512)
+    for nm in ("wb", "wc"):
+        for h in range(8):
+            i = io(T[nm][:, 536 * h:536 * h + 536], [[0, 536]], 0, 0, [nm], 536)
+            ops[i]["after"] = o
+            o = i
 
-    def unfold(k, src, c0, r):
-        return dma([(WT[k % 2][4 * c::16, 0:W], src[:, c0 + 256 * c:c0 + 256 * c + 256]) for c in range(4)], r, ["w%d" % (k % 2)], 700000)
+    def unfold(k, extra):
+        c0 = 1024 * (k - 1)
+        dma([(WT[k][4 * c::16, 0:W], T.tl[:, c0 + 256 * c:c0 + 256 * c + 256]) for c in range(4)], ["tl%d" % k] + extra, [WN[k], "un%d" % k], 524288)
 
     def send_table(k, extra):
-        o = remote([(T.lf[:, :], [(k, T.tl[:, 1024 * (k - 1):1024 * k])], 0, ne, "rt%d" % k)], ["lf"] + extra, 524288)
+        o = remote([(T.lf[:, :], [(k, T.tl[:, 1024 * (k - 1):1024 * k])], 0, ne, "rt%d" % k)], ["lf0", "lf1"] + extra, 524288)
         recv("rt%d" % k, ne, ["tl%d" % k], o)
 
-    unfold(0, T.lf, 0, ["lf", "w0f0", "w0f1", "w0f2", "w0f3"])
+    def pass_table(k):
+        dma([(T.tf[:, 256 * c:256 * c + 256], WT[k - 1][4 * c::16, 0:W]) for c in range(4)], [WN[k - 1]], ["tf"], 524288)
+        o = remote([(T.tf[:, :], [(1, T.tl[:, 1024 * (k - 1):1024 * k])], 0, ne, "rt%d" % k)], ["tf"], 524288, local="rf%d" % k)
+        recv("rt%d" % k, ne, ["tl%d" % k], o)
+        recv("rf%d" % k, ne, ["tf"], o)
+
+    def copy_window(c, extra):
+        dma([(T.wv[:, W * c:W * c + W], T.wv[:, 0:W])], ["wvm0", "wvm1", "wvr"] + extra, ["wv%d" % c], 1048576)
+
     send_table(1, ["wvr"])
-    for h in range(4):
-        i = io(T.w1[:, 1072 * h:1072 * h + 1072], [[0, 1072]], 0, 0, ["w1"], 1072)
-        ops[i]["after"] = o
-    unfold(1, T.tl, 0, ["tl1"])
-    dma([(T.wv[:, W * c:W * c + W], T.wv[:, 0:W]) for c in range(1, 4)], ["wvm", "wvr"], ["wv1"], 3200000)
+    copy_window(1, [])
+    copy_window(2, ["wv1"])
+    unfold(1, ["wv1"])
+    copy_window(3, ["wv2"])
+    last = "wv3"
+    for k in range(2, ST + 1):
+        if k not in CHAIN:
+            send_table(k, [last])
+            last = "tl%d" % k
+            if k == 2:
+                unfold(2, [])
+                last = "un2"
 
     def scatter(s, d):
+        if (s, d) not in lists:
+            return
         tag[0] = "s%d%d" % (s, d)
         k = d + s - 1
         i = DELTAS.index((s, d))
-        win = WT[k % 2]
+        win = WT[k]
         op("V", lambda: V.tensor_copy(win[:, 0:TWW].indirect(T.dl[:, DLW * i + K:DLW * i + K + 12]), T.dl[:, DLW * i:DLW * i + K]),
-           ["dl%d%d" % (s, d)], ["w%d" % (k % 2)], 50 + K * SCC, kind="s")
+           ["dl%d%d" % (s, d)], [WN[k]], 50 + K * SCC * CY, kind="s")
 
-    ts(EE[0][:, :], T.owi[:, :], -2048.0, None, A.add, None, ["owi"], ["e0_0", "e0_1"], K)
-    mm([(PX[1][:, 0:12], T.zl[:, 15 - a:143 - a], EE[0][:, a::16], a == 0, a == 15, 64) for a in range(16)],
-       ["zl", "e0_0", "e0_1"], ["#w14"])
-    cp(O["mc"], PX[1][:, 0:12], [], ["#w14", "mc"], 12)
-    cp(T.uu[:, :], T.imgi[:, :], ["imgi"], ["u0", "u1"], K)
-    ts(T.bc[:, :], T.imgi[:, :], -2048.0, None, A.add, None, ["imgi"], ["bc0", "bc1"], K)
-
-    def gather(b, win, wr, out, nm):
-        for l0 in range(LB * b, LB * b + LB, GL):
-            o_, i_ = out[:, 16 * l0:16 * (l0 + GL)], win.indirect(T.uu[:, l0:l0 + GL])
-            op("X", (lambda o_=o_, i_=i_: V.tensor_copy(o_, i_), lambda o_=o_, i_=i_: S.activation(o_, i_, F.Identity)),
-               wr + ["u%d" % b], [nm + "_%d" % (l0 // GL)], 60 + 16 * GL * GC, kind="g")
+    xs(EE[0][:, :], T.owi[:, :], 1.0, -2048.0, ["owi"], ["e0_0", "e0_1"], K)
+    mm([(PX[1][:, 256:268], T.zl[:, 15 - a:143 - a], EE[0][:, a::16], a == 0, a == 15, 64) for a in range(16)],
+       ["zl", "e0_0", "e0_1"], ["#w1"])
+    xs(T.mc[:, :], PX[1][:, 256:268], 1.0, 0.0, [], ["#w1", "mc"], 12)
+    lead[0] = 20000.0
+    xs(T.uu[:, :], T.imgi[:, :], 1.0, 0.0, ["imgi"], ["u_%d" % k for k in range(K // 16)], K)
+    lead[0] = 0.0
+    xs(T.bc[:, :], T.imgi[:, :], 1.0, -2048.0, ["imgi"], ["bc0", "bc1"], K)
 
     def pieces(nm, l0, l1):
-        return [nm + "_%d" % k for k in range(l0 // GL, (l1 + GL - 1) // GL)]
+        return [nm + "_%d" % k for k in range(l0 // 16, l1 // 16)]
 
+    def gather(b, win, wr, out, nm, key):
+        l0 = LB * b
+        for gl in PAR["CUT"][key[2]]:
+            o_, i_ = out[:, 16 * l0:16 * (l0 + gl)], win.indirect(T.uu[:, l0:l0 + gl])
+            if key[0]:
+                fns = (lambda o_=o_, i_=i_: V.tensor_copy(o_, i_), lambda o_=o_, i_=i_: S.activation(o_, i_, F.Identity))
+            else:
+                fns = (lambda o_=o_, i_=i_: V.tensor_scalar(o_, i_, -127.5, None, A.add),
+                       lambda o_=o_, i_=i_: S.activation(o_, i_, F.Identity, bias=-127.5))
+            who = PAR["WHO"].get((key, len(gathers.get(key, []))), "X")
+            i = op(who, fns if who == "X" else fns[who == "S"], wr + pieces("u", l0, l0 + gl), pieces(nm, l0, l0 + gl),
+                   60 + 16 * gl * GC * CY, kind="g", after=made if who == "S" and not key[0] else None)
+            gathers.setdefault(key, []).append(i)
+            l0 += gl
+
+    tag[0] = "f0"
     for b in range(NB):
-        gather(b, T.tw[:, 0:W], ["tw"], T.ff, "f0")
+        gather(b, T.tw[:, 0:W], ["tw"], T.ff, "ff", (0, b, 3))
+    rounder = {}
+    HALF = PAR["HALF"]
 
-    def to_list(b, add, plain):
-        ls = slice(LB * b, LB * b + LB)
-        x = "#x%d" % b
-        u = ["u%d" % b]
+    def begin(s, ch):
+        src, r = (T.th, ["th%d" % ch]) if s - 1 in HALF else (T.ff, pieces("ff", 32 * ch, 32 * ch + 32))
+        rows = 2 if s == ST else 1
+
+        def fn():
+            lift = s == ST or ops[rounder[(s, ch)]]["e"] == "S"
+            if lift:
+                P.matmul(PF[ch][:, :], T.one[0:rows, 0:128], T.c49[0:rows, :], True, False)
+            return P.matmul(PF[ch][:, :], T.idb[:, :], src[:, 512 * ch:512 * ch + 512], not lift, False)
+        op("P", fn, ["one", "c49", "idb"] + r, ["#f%d" % ch], (1024 if s == ST or ch in PAR["KS"] else 512) * PC)
+
+    def to_list(b, add, plain, l0=0, l1=LB):
+        ls = slice(LB * b + l0, LB * b + l1)
+        x = pieces("#x%d" % b, l0, l1)
+        u, yi, ya = [pieces(nm, LB * b + l0, LB * b + l1) for nm in ("u", "yi", "ya")]
         if plain:
-            ts(T.uu[:, ls], PX[b][:, 0:LB], add, None, A.add, None, [], [x] + u, LB)
+            xs(T.uu[:, ls], PX[b][:, l0:l1], 1.0, add, [], x + u, l1 - l0)
         else:
-            ts(T.yi[:, ls], PX[b][:, 0:LB], add, None, A.add, None, [], [x, "yi%d" % b], LB)
-            ts(T.ya[:, ls], T.yi[:, ls], W - 1, None, A.bitwise_and, None, ["yi%d" % b], ["ya%d" % b], LB)
-            cp(T.uu[:, ls], T.ya[:, ls], ["ya%d" % b], u, LB)
+            xs(T.yi[:, ls], PX[b][:, l0:l1], 1.0, add, [], x + yi, l1 - l0)
+            ts(T.ya[:, ls], T.yi[:, ls], W - 1, None, A.bitwise_and, None, yi, ya, l1 - l0)
+            xs(T.uu[:, ls], T.ya[:, ls], 1.0, 0.0, ya, u, l1 - l0)
 
     def choose(s, b):
         tag[0] = "c%d%d" % (s, b)
         ls = slice(LB * b, LB * b + LB)
-        x = "#x%d" % b
+        x = pieces("#x%d" % b, 0, LB)
         X = PX[b]
         c0 = 16 * LB * b
-        fr = ["ff%d" % ch for ch in range(3 * b, 3 * b + 3)] + pieces("f0", LB * b, LB * b + LB)
+        if s - 1 in HALF:
+            parts = [(T.th, T.wk[:, 0:8]), (T.kk, T.wk[:, 8:16])]
+            fr = [nm + "%d" % ch for ch in range(3 * b, 3 * b + 3) for nm in ("th", "kk")]
+        else:
+            parts, fr = [(T.ff, T.wk[:, 0:8])], pieces("ff", LB * b, LB * b + LB)
         mm([(X[0:LB, 0:256], T.one[0:1, 0:LB], T.c15[0:1, :], True, False, 256)]
-           + [(X[0:LB, i:256:32], T.ff[:, c0 + i:c0 + 16 * LB:16], T.wk[:, :], False, i == 15, 64) for i in range(16)],
-           ["one", "c15", "wk"] + fr, [x])
-        scan(T.rm[0:LB, 256 * b:256 * b + 256], T.rs[0:LB, :], X[0:LB, 0:256], -2.0 ** 20, A.add, A.max, ["rs"], [x, "rm%d" % b], 256)
+           + [(X[0:LB, i:256:32], f_[:, c0 + i:c0 + 16 * LB:16], w_, False, i == 15 and f_ is parts[-1][0], 64)
+              for (f_, w_) in parts for i in range(16)], ["one", "c15", "wk", "wkn"] + fr, x)
+        scan(T.rm[0:LB, 256 * b:256 * b + 256], T.rs[0:LB, :], X[0:LB, 0:256], -2.0 ** 20, A.add, A.max, ["rs"], x + ["rm%d" % b], 256)
         tt(T.mk[0:LB, 256 * b:256 * b + 240], X[0:LB, 0:240], T.rm[0:LB, 256 * b + 16:256 * b + 256], A.is_equal,
-           ["rm%d" % b], [x, "mk%d" % b], 240, 1.0)
+           ["rm%d" % b], x + ["mk%d" % b], 240, 1.0)
         mm([(X[:, 0:LB], T.mk[0:LB, 256 * b:256 * b + 128], T.idb[0:LB, 0:LB], True, False, LB),
-            (X[:, 0:LB], T.mk[0:LB, 256 * b + 112:256 * b + 240], T.idb[0:LB, 0:LB], False, True, LB)], ["mk%d" % b, "idb"], [x])
-        tt(T.mb[:, ls], X[:, 0:LB], T.bc[:, ls], A.mult, ["bc%d" % b], [x, "mb%d" % b], LB, 1.0)
+            (X[:, 0:LB], T.mk[0:LB, 256 * b + 112:256 * b + 240], T.idb[0:LB, 0:LB], False, True, LB)], ["mk%d" % b, "idb"], x)
+        tt(T.mb[:, ls], X[:, 0:LB], T.bc[:, ls], A.mult, ["bc%d" % b], x + ["mb%d" % b], LB, 1.0)
         nc = LB // 16
-        mm([(X[:, 0:nc], T.zo[:, 15 - a:143 - a], T.mb[:, LB * b + a:LB * b + LB:16], a == 0, a == 15, 64) for a in range(16)]
-           + [(X[:, 128:128 + LB], T.bd[:, :], T.mb[:, ls], True, True, LB)], ["zo", "bd", "mb%d" % b], [x])
+        mm([(X[:, 0:nc], T.zo[:, 15 - a:143 - a], T.mb[:, LB * b + a:LB * b + LB:16], a == 0, a == 15, 64) for a in range(16)],
+           ["zo", "mb%d" % b], x)
         os_ = slice(nc * b, nc * b + nc)
-        ts(T.wo[:, os_], X[:, 0:nc], 2048.0, None, A.add, None, [], [x, "wo%d" % b], nc)
+        xs(T.wo[:, os_], X[:, 0:nc], 1.0, 2048.0, [], x + ["wo%d" % b], nc)
         E = EE[s % 2]
-        win = WT[(s - 1) % 2]
-        op("V", lambda: V.tensor_scalar(E[:, ls], win[:, 0:TWW].indirect(T.wo[:, os_]), -2048.0, None, A.add),
-           ["wo%d" % b, "w%d" % ((s - 1) % 2)], ["e%d_%d" % (s % 2, b)], 50 + LB * GC, kind="g")
-        xs(T.wf[:, os_], X[:, 0:nc], 1.0, 0.0, [], [x, "wf%d" % b], nc)
-        xs(T.wr[:, ls], X[:, 128:128 + LB], 1.0, 0.0, [], [x, "wr%d" % b], LB)
-        xs(T.wn[:, os_], T.wf[:, os_], -16384.0, 0.0, ["wf%d" % b], ["wn%d" % b], nc)
-        mm([(X[:, 0:LB], T.idh[:, :], T.bc[:, ls], True, False, LB), (X[:, 0:LB], T.bda[:, 0:128], E[:, ls], False, True, LB)],
-           ["idh", "bc%d" % b, "bda0", "e%d_%d" % (s % 2, b)], [x])
+        xs(E[:, ls], WT[s - 1][:, 0:W].indirect(T.wo[:, os_]), 1.0, -2048.0, ["wo%d" % b, WN[s - 1]], ["e%d_%d" % (s % 2, b)], LB + 12, GC, "g")
+        mm([(X[:, 0:LB], T.idb[:, :], T.bc[:, ls], True, False, LB), (X[:, 0:LB], T.bda[:, 0:128], E[:, ls], False, True, LB)],
+           ["idb", "bc%d" % b, "bda0", "e%d_%d" % (s % 2, b)], x)
         to_list(b, 6144.0, 3 * (s - 1) >= PLAIN)
 
     def winners(s):
         tag[0] = "w%d" % s
+        lead[0] = PAR["WB"]
         E, Ep = EE[s % 2], EE[(s - 1) % 2]
-        X, xw = PX[BK[0]], "#w%d1" % BK[0]
-        mm([(X[:, 256:268], T.zl[:, 15 - a:143 - a], E[:, a::16], a == 0, a == 15, 64) for a in range(16)],
-           ["zl"] + ["e%d_%d" % (s % 2, b) for b in range(NB)], [xw])
-        xs(O["lc"], X[:, 256:268], 1.0, 0.0, [], [xw, "lc"], 12)
-        tt(O["nc"], O["mc"], O["lc"], A.is_ge, ["mc", "lc"], ["nc"], 12)
-        xs(O["x"], O["nc"], 8192.0, -2048.0, ["nc"], ["x"], 12)
-        tt(T.oh[:, 0:12], O["mc"], O["x"], A.max, ["mc", "x"], ["oh0"], 12)
-        ts(T.oh[:, 12:24], T.oh[:, 0:12], -1.0, None, A.mult, None, ["oh0"], ["oh1"], 12)
-        X, xw = PX[BK[1]], "#w%d2" % BK[1]
-        mm([(X[:, 0:193], T.idb[:, :], T.zz[:, 0:193], True, False, 193)]
-           + [(X[:, a:192:16], T.bda[:, 128 * a:128 * a + 128], T.oh[:, 12:24], False, False, 64) for a in range(16)]
-           + [(X[:, a + 1:193:16], T.bda[:, 128 * a:128 * a + 128], T.oh[:, 0:12], False, a == 15, 64) for a in range(16)],
-           ["idb", "zz", "oh0", "oh1"] + BDA, [xw])
+        es, ep = [["e%d_%d" % (x % 2, b) for b in range(NB)] for x in (s, s - 1)]
+        X, xw = PX[BK[0]][:, 256:512], "#w%d" % BK[0]
+        if s == 1:
+            mm([(X[:, 0:K], T.bdl[:, 0:128], Ep[:, :], True, True, K)], ["bdl"] + ep, [xw])
+        else:
+            mm([(X[:, a:192:16], T.bda[:, 128 * a:128 * a + 128], T.mc[:, :], True, True, 64) for a in range(16)], ["mc"] + BDA, [xw])
+        xs(T.kr[:, 1:193], X[:, 0:K], 1.0, 0.0, [], [xw, "kr"], K)
+        mm([(X[:, 0:K], T.ide[:, :], Ep[:, :], True, False, K), (X[:, 0:K], T.idl[:, :], T.kr[:, 1:193], False, True, K)],
+           ["ide", "idl", "kr"] + ep, [xw])
+        xs(T.sv[:, DLW * (s - 1):DLW * (s - 1) + K], X[:, 0:K], 1.0, cc[:, 16 + s:17 + s], ["svc%d" % s], [xw, "sv%da" % s], K)
+        mm([(X[:, 0:K], T.bdb[:, :], T.mb[:, :], True, True, K)], ["bdb", "mb0", "mb1"], [xw])
+        xs(T.wr[:, :], X[:, 0:K], 1.0, 0.0, [], [xw, "wr"], K)
+        xs(T.wf[:, :], T.wo[:, :], 1.0, -2048.0, ["wo0", "wo1"], ["wf"], 12)
+        X, xw = PX[BK[1]][:, 256:512], "#w%d" % BK[1]
+        mm([(X[:, 0:193], T.idb[:, :], T.kr[:, 0:193], True, False, 193), (X[:, 0:K], T.idn[:, :], T.kr[:, 1:193], False, False, K)]
+           + ([(X[:, 192:193], T.one[0:1, 0:128], T.c3[0:1, s - 1:s], False, False, 64)] if s > 1 else [])
+           + [(X[:, 0:K], T.bdl[:, 0:128], E[:, :], False, False, K), (X[:, 1:193], T.bdl[:, 128:256], E[:, :], False, True, K)],
+           ["idb", "idn", "kr", "kr0", "one", "c3", "bdl", "bdn"] + es, [xw])
         xs(T.dd[:, 0:193], X[:, 0:193], 1.0, -1.0 / 256, [], [xw, "dd"], 193)
-        X, xw = PX[BK[2]], "#w%d3" % BK[2]
-        mm([(X[:, 256:448], T.ide[:, :], Ep[:, :], True, False, K)]
-           + [(X[:, 256 + a:448:16], T.bdl[:, 128 * a:128 * a + 128], T.oh[:, 0:12], False, a == 15, 64) for a in range(16)],
-           ["ide", "oh0"] + ["e%d_%d" % ((s - 1) % 2, b) for b in range(NB)] + BDL, [xw])
-        ts(T.sv[:, DLW * (s - 1):DLW * (s - 1) + K], X[:, 256:448], 2048.0, None, A.add, None, [], [xw, "sv%da" % s], K)
         for c in range(12):
-            e_ = T.ee[:, 194 * c:194 * c + K]
-            op("X", (lambda c=c, e_=e_: V.tensor_scalar(e_, T.wr[:, :], T.wf[:, c:c + 1], 16384.0, A.not_equal, A.mult),
-                     lambda c=c, e_=e_: S.activation(e_, T.wr[:, :], F.Abs, bias=T.wn[:, c:c + 1], scale=16384.0)),
-               ["wr0", "wr1", "wf%d" % (c // 6), "wn%d" % (c // 6)], ["ee%d" % c], vc(K))
+            ts(T.ee[:, 194 * c:194 * c + K], T.wr[:, :], T.wf[:, c:c + 1], 16384.0, A.not_equal, A.mult, ["wr", "wf"], ["ee%d" % c], K, 0.5)
         for c in range(12):
             scan(T.sc[:, 194 * c:194 * c + 193], T.dd[:, 0:193], T.ee[:, 194 * c:194 * c + 193], 16384.0, A.add, A.min,
                  ["dd", "ee%d" % c, "eec"], ["sc%d" % c], 193)
-        tt(O["ko"], O["mc"], O["jo"], A.add, ["mc", "jo"], ["ko"], 12)
-        tt(O["a"], T.wf[:, :], O["d1"], A.subtract, ["wf0", "wf1", "d1"], ["a"], 12)
-        tt(O["win"], T.sc[:, 192::194], O["ko"], A.is_equal, ["ko"] + ["sc%d" % c for c in range(12)], ["win"], 12)
+        tt(O["a"], T.wf[:, :], O["d1"], A.subtract, ["wf", "d1"], ["a"], 12)
+        tt(O["x"], T.sc[:, 192::194], O["jo"], A.subtract, ["jo"] + ["sc%d" % c for c in range(12)], ["x"], 12)
+        ts(O["dm"], O["x"], 1.5 * 2 ** 23, 1.5 * 2 ** 23, A.add, A.subtract, ["x"], ["dm"], 12)
+        tt(O["win"], O["x"], O["dm"], A.is_equal, ["x", "dm"], ["win"], 12)
         tt(O["b"], O["a"], O["win"], A.mult, ["a", "win"], ["b"], 12)
         tt(O["c"], O["b"], O["d2"], A.add, ["b", "d2"], ["c"], 12)
-        cp(T.sv[:, DLW * (s - 1) + K:DLW * (s - 1) + K + 12], O["c"], ["c"], ["sv%db" % s], 12)
-        ds = [d for (s2, d) in DELTAS if s2 == s]
+        xs(T.sv[:, DLW * (s - 1) + K:DLW * (s - 1) + K + 12], O["c"], 1.0, 0.0, ["c"], ["sv%db" % s], 12)
+        ds = [d for (s2, d) in lists if s2 == s]
         k = ne // {1: 1, 2: 2, 3: 4, 4: 4}[len(ds)]
         src = T.sv[:, DLW * (s - 1):DLW * s]
-        o = remote([(src, [(d, T.dl[:, DLW * DELTAS.index((s, d)):DLW * (DELTAS.index((s, d)) + 1)])], k * (d - 1), k, "rd%d%d" % (s, d))
-                    for d in ds], ["sv%da" % s, "sv%db" % s], 60000)
+        o = remote([(src, [(d, T.dl[:, DLW * DELTAS.index((s, d)):DLW * (DELTAS.index((s, d)) + 1)])], k * j, k, "rd%d%d" % (s, d))
+                    for j, d in enumerate(ds)], ["sv%da" % s, "sv%db" % s], 50000 * len(ds))
         for d in ds:
             recv("rd%d%d" % (s, d), k, ["dl%d%d" % (s, d)], o)
+        lead[0] = 0.0
         if s < ST:
-            tt(O["dm"], O["lc"], O["mc"], A.subtract, ["lc", "mc"], ["dm"], 12)
-            xs(O["m3"], O["mc"], 1.0, 3.0, ["mc"], ["m3"], 12)
             tt(O["b2"], O["dm"], O["win"], A.mult, ["dm", "win"], ["b2"], 12)
-            tt(O["mc"], O["m3"], O["b2"], A.add, ["m3", "b2"], ["mc"], 12)
+            tt(T.mc[:, :], T.mc[:, :], O["b2"], A.subtract, ["b2"], ["mc"], 12)
 
     def letter(s, q, b):
         tag[0] = "l%d%d%d" % (s, q, b)
         ls = slice(LB * b, LB * b + LB)
-        G = GG[(3 * s + q) % 2]
-        gn = "g%d" % ((3 * s + q) % 2)
+        G = GG[(q + 1) % 3]
+        gn = "g%d" % ((q + 1) % 3)
         if 3 * (s - 1) + q < PLAIN:
-            gather(b, T.wv[:, 0:W], ["wvm", "wvr"], G, gn)
+            gather(b, T.wv[:, 0:W], ["wvm0", "wvm1", "wvr"], G, gn, (s, b, q))
         else:
-            gather(b, T.wv[:, 0:4 * W], ["wvm", "wvr", "wv1"], G, gn)
+            gather(b, T.wv[:, 0:4 * W], ["wvm0", "wvm1", "wvr", "wv1", "wv2", "wv3"], G, gn, (s, b, q))
         X = PX[b]
-        c0 = 16 * LB * b
-        mm([(X[:, 0:LB], T.sd[:, 128 * q:128 * q + 128], EE[s % 2][:, ls], True, False, LB)]
-           + [(X[:, 0:LB], T.zd[:, 15 - i:143 - i], G[:, c0 + i:c0 + 16 * LB:16], False, i == 15, LB) for i in range(16)],
-           ["sd%d" % q, "e%d_%d" % (s % 2, b), "zd"] + pieces(gn, LB * b, LB * b + LB), ["#x%d" % b])
+        for (l0, l1) in ([(0, LB // 2), (LB // 2, LB)] if (b, q) in PAR["SPLIT"] else [(0, LB)]):
+            g0, g1 = LB * b + l0, LB * b + l1
+            mm([(X[:, l0:l1], T.sd[:, 128 * q:128 * q + 128], EE[s % 2][:, g0:g1], True, False, max(64, l1 - l0))]
+               + [(X[:, l0:l1], T.zd[:, 15 - i:143 - i], G[:, 16 * g0 + i:16 * g1:16], False, i == 15, max(64, l1 - l0)) for i in range(16)],
+               ["sd%d" % q, "e%d_%d" % (s % 2, b), "zd"] + pieces(gn, g0, g1), pieces("#x%d" % b, l0, l1))
+            if q < 2:
+                to_list(b, 8192.0, 3 * (s - 1) + q + 1 >= PLAIN, l0, l1)
         for ch in range(3 * b, 3 * b + 3):
             cs = slice(512 * ch, 512 * ch + 512)
-            if q == 0:
-                mm([(PF[ch][:, :], T.one[0:1, 0:128], T.c49[0:1, :], True, False, 512), (PF[ch][:, :], T.idb[:, :], T.ff[:, cs], False, False, 512)],
-                   ["one", "c49", "idb", "ff%d" % ch] + pieces("f0", 32 * ch, 32 * ch + 32), ["#f%d" % ch])
-            mm([(PF[ch][:, :], T.idb[:, :], G[:, cs], False, q == 2, 512)], ["idb"] + pieces(gn, 32 * ch, 32 * ch + 32), ["#f%d" % ch])
+            if q == 0 and s not in HALF:
+                begin(s, ch)
+            mm([(PF[ch][:, :], T.idb[:, :], G[:, cs], q == 0 and s in HALF, q == 2, 512)], ["idb"] + pieces(gn, 32 * ch, 32 * ch + 32), ["#f%d" % ch])
         if q < 2:
-            to_list(b, 8192.0, 3 * (s - 1) + q + 1 >= PLAIN)
             return
-        ts(T.yi[:, ls], X[:, 0:LB], 8192.0, None, A.add, None, [], ["#x%d" % b, "yi%d" % b], LB)
-        ts(T.ya[:, ls], T.yi[:, ls], W - 1, None, A.bitwise_and, None, ["yi%d" % b], ["ya%d" % b], LB)
+        yi, ya = pieces("yi", LB * b, LB * b + LB), pieces("ya", LB * b, LB * b + LB)
+        xs(T.yi[:, ls], X[:, 0:LB], 1.0, 8192.0, [], pieces("#x%d" % b, 0, LB) + yi, LB)
+        ts(T.ya[:, ls], T.yi[:, ls], W - 1, None, A.bitwise_and, None, yi, ya, LB)
         if s < ST:
-            ts(T.bc[:, ls], T.ya[:, ls], -2048.0, None, A.add, None, ["ya%d" % b], ["bc%d" % b], LB)
+            xs(T.bc[:, ls], T.ya[:, ls], 1.0, -2048.0, ya, ["bc%d" % b], LB)
         else:
-            cp(T.yo[:, ls], T.ya[:, ls], ["ya%d" % b], ["yo%d" % b], LB)
+            xs(T.yo[:, ls], T.ya[:, ls], 1.0, 0.0, ya, ["yo%d" % b], LB)
             dma([(T.yimg[:, ls], T.yo[:, ls])], ["yo%d" % b], [], 50000)
+        tag[0] = "k%d%d" % (s, b)
         for ch in range(3 * b, 3 * b + 3):
             cs = slice(512 * ch, 512 * ch + 512)
-            xs(T.kk[:, cs], PF[ch][:, :], 1.0, -127.5, [], ["#f%d" % ch, "kk%d" % ch], 512)
-            tt(T.ff[:, cs], PF[ch][:, :], T.kk[:, cs], A.subtract, ["kk%d" % ch], ["#f%d" % ch, "ff%d" % ch, "f0_%d" % ch], 512, 1.0)
+            k_, f_ = T.kk[:, cs], PF[ch][:, :]
+            fn = pieces("ff", 32 * ch, 32 * ch + 32)
+            if s in HALF:
+                tt(T.th[:, cs], f_, T.ff[:, cs], A.add, fn, ["#f%d" % ch, "th%d" % ch], 512, 1.0)
+                ts(k_, T.th[:, cs], 1.5 * 2 ** 31, 1.5 * 2 ** 31, A.add, A.subtract, ["th%d" % ch], ["kk%d" % ch], 512, 0.5)
+                continue
             if s == ST:
-                dma([(T.yf[:, cs], T.ff[:, cs])], ["ff%d" % ch], [], 131072)
+                xs(k_, f_, 1.0, -127.5, [], ["#f%d" % ch, "kk%d" % ch], 512)
+            else:
+                rounder[(s, ch)] = op("X" if ch in PAR["KS"] else "Y", (lambda k_=k_, f_=f_: V.tensor_scalar(k_, f_, 1.5 * 2 ** 31, 1.5 * 2 ** 31, A.add, A.subtract),
+                                            lambda k_=k_, f_=f_: S.activation(k_, f_, F.Identity)), [], ["#f%d" % ch, "kk%d" % ch], vc(512))
+            tt(T.ff[:, cs], PF[ch][:, :], T.kk[:, cs], A.subtract, ["kk%d" % ch], ["#f%d" % ch] + fn, 512, 1.0)
+            if s == ST:
+                dma([(T.yf[:, cs], T.ff[:, cs])], fn, [], 131072)
 
     for s in range(1, ST + 1):
         if s > 1:
             scatter(s - 1, 1)
+        if s in CHAIN:
+            pass_table(s)
         for b in range(NB):
             choose(s, b)
-        if s < ST:
-            if s == 1:
-                for k in range(2, 5):
-                    send_table(k, ["e1_0", "tl1"])
-            unfold(s + 1, T.tl, 1024 * s, ["tl%d" % (s + 1)])
+        if s in CHAIN:
+            unfold(s, [])
+        if s in (2, 3) and s + 1 not in CHAIN:
+            unfold(s + 1, [])
             for s2 in range(1, s):
                 scatter(s2, s + 2 - s2)
         winners(s)
@@ -428,174 +520,160 @@ def build(g, T, topo, rank):
             for b in range(NB):
                 letter(s, q, b)
     scatter(ST, 1)
-    dma([(T.yent[:, W * c:W * c + W], T.w0[4 * c::16, 0:W]) for c in range(3)] + [(T.yelen[:, :], T.w0[12::16, 0:W])], ["w0"], [], 600000)
-    ops[3]["after"] = 0
-    ops[4]["after"] = 3
+    dma([(T.yent[:, W * c:W * c + W], T.wc[4 * c::16, 0:W]) for c in range(3)] + [(T.yelen[:, :], T.wc[12::16, 0:W])], ["wc"], [], 524288)
+    chain = [i for s in range(1, ST + 1) for (b, q) in PAR["ORDER"] for i in gathers[(s, b, q)]]
+    for i, j in zip(chain, chain[1:]):
+        ops[j]["behind"] = i
     return ops, rloc[0]
 
 
 def plan(ops):
     nops = len(ops)
-    state = [SEED * 7919 + 1]
+    state = [PAR["SEED"] * 7919 + 1]
 
     def rnd():
         state[0] = (state[0] * 1103515245 + 12345) % 2147483648
         return state[0] / 2147483648.0
-    lean = {}
-    for o in ops:
-        if o["tag"] not in lean:
-            lean[o["tag"]] = JT * (rnd() - 0.5)
     lastw, readers = {}, {}
-    pred = [dict() for _ in ops]
+    pred0 = [dict() for _ in ops]
     for i, o in enumerate(ops):
         if o["after"] is not None:
-            pred[i][o["after"]] = 0
+            pred0[i][o["after"]] = 0
         for w in o["w"]:
             for j in readers.get(w, []) + ([lastw[w]] if w in lastw else []):
-                pred[i][j] = max(pred[i].get(j, 0), 1 if w[0] == "#" else 2)
+                pred0[i][j] = max(pred0[i].get(j, 0), 1 if w[0] == "#" else 2)
         for r in o["r"]:
             if r in lastw:
-                pred[i][lastw[r]] = 2
+                pred0[i][lastw[r]] = 2
         for r in o["r"]:
             readers.setdefault(r, []).append(i)
         for w in o["w"]:
             lastw[w] = i
             readers[w] = []
-
-    def hard(i, j, e):
-        k = pred[i][j]
-        return k == 2 or (k == 1 and ops[j]["e"] != e)
-
-    def gap(i, j, e):
-        if pred[i][j] == 0 and ops[i]["e"] == ops[j]["e"]:
-            return -ops[j]["lat"]
-        return LAT if hard(i, j, e) else 0.0
+    for i, o in enumerate(ops):
+        if o["behind"] is not None and o["behind"] not in pred0[i]:
+            pred0[i][o["behind"]] = -1
     succ = [[] for _ in ops]
     for i in range(nops):
-        for j in pred[i]:
+        for j in pred0[i]:
             succ[j].append(i)
-    prio = [0.0] * nops
-    for i in range(nops - 1, -1, -1):
-        prio[i] = ops[i]["c"] + ops[i]["lat"] + LAT + max([prio[k] for k in succ[i]] + [0.0])
-    for i in range(nops):
-        prio[i] += ops[i]["bias"] + JG * rnd() + lean[ops[i]["tag"]]
-    left = [len(pred[i]) for i in range(nops)]
-    ready = [i for i in range(nops) if left[i] == 0]
-    done = [0.0] * nops
-    free, base, size = {}, {}, {}
-    for o in ops:
-        size[o["bank"]] = size.get(o["bank"], 0) + 1
-    held = {0: None, 1: None}
-    users = {0: [], 1: []}
-    while ready:
-        cand = []
-        for i in ready:
-            bk = ops[i]["bank"]
-            if bk is not None and held[bk[0]] not in (None, bk):
-                continue
-            for e in ("VS" if ops[i]["e"] == "X" else ops[i]["e"]):
-                if (i, e) not in base:
-                    base[(i, e)] = max([done[j] + gap(i, j, e) for j in pred[i]] + [0.0])
-                t = base[(i, e)] if e == "R" else max(base[(i, e)], free.get(e, 0.0))
-                if bk is not None and bk[1] == i:
-                    t = max([t] + [done[j] + LAT for j in users[bk[0]] if ops[j]["e"] != e])
-                cand.append((t + (VPEN if ops[i]["e"] == "X" and e == "V" else 0.0), -prio[i], i, e, t))
-        best = min(cand)
-        e = best[3]
-        if e != "R":
-            best = min([c for c in cand if c[3] == e and c[0] <= best[0] + WIN], key=lambda c: c[1])
-        i, t = best[2], best[4]
-        ops[i]["e"] = e
-        ready.remove(i)
-        bk = ops[i]["bank"]
-        if bk is not None:
-            if bk[1] == i:
-                for j in users[bk[0]]:
-                    pred[i][j] = max(pred[i].get(j, 0), 1)
-                users[bk[0]] = []
-            users[bk[0]].append(i)
-            size[bk] -= 1
-            held[bk[0]] = bk if size[bk] else None
-        if e != "R":
-            free[e] = t + ops[i]["c"]
-        done[i] = t + ops[i]["c"] + ops[i]["lat"]
+    line, cnt = [i for i in range(nops) if not pred0[i]], [len(pred0[i]) for i in range(nops)]
+    for i in line:
         for k in succ[i]:
-            left[k] -= 1
-            if left[k] == 0:
-                ready.append(k)
-    for i in range(nops):
-        succ[i] = []
-    for i in range(nops):
-        for j in pred[i]:
-            succ[j].append(i)
+            cnt[k] -= 1
+            if cnt[k] == 0:
+                line.append(k)
+    cost, lat, nb = [o["c"] for o in ops], [o["lat"] for o in ops], [o["bytes"] for o in ops]
+    LAT, BW, WIN = PAR["LAT"], PAR["BW"], PAR["WIN"]
+    level = [0.0] * nops
+    for i in line[::-1]:
+        level[i] = cost[i] + lat[i] + nb[i] / BW + LAT + max([level[k] for k in succ[i]] + [0.0])
 
-    def place(key, back):
-        before, after = (succ, pred) if back else (pred, succ)
-        cnt = [len(before[i]) for i in range(nops)]
-        rdy = [i for i in range(nops) if cnt[i] == 0]
-        busy = {e: [] for e in "VSPGQ"}
-        st, en = [0.0] * nops, [0.0] * nops
-        while rdy:
-            i = min(rdy, key=lambda k: key[k])
-            rdy.remove(i)
-            o = ops[i]
-            best = None
-            for e in ("SV" if o["free"] else o["e"]):
-                o["e"] = e
-                t = max([en[j] + (gap(j, i, ops[j]["e"]) if back else gap(i, j, e)) for j in before[i]] + [0.0])
-                if back:
-                    t += o["lat"]
-                pos = 0
-                if e != "R":
-                    b = busy[e]
-                    pos = len(b)
-                    while pos > 0 and b[pos - 1][1] > t:
-                        pos -= 1
-                    while pos < len(b) and t + o["c"] > b[pos][0]:
-                        t = max(t, b[pos][1])
-                        pos += 1
-                if best is None or t + VPEN < best[0]:
-                    best = (t, e, pos)
-            t, e, pos = best
-            o["e"] = e
+    def greedy(lean, vpen):
+        pred = [dict(p) for p in pred0]
+        prio = [level[i] + ops[i]["bias"] + lean[i] for i in range(nops)]
+        left = [len(p) for p in pred]
+        ready = [i for i in range(nops) if left[i] == 0]
+        start, done, eng = [0.0] * nops, [0.0] * nops, [o["e"] for o in ops]
+        free, base = {e: 0.0 for e in "VSPGQD"}, {}
+        users, order = {0: {}, 1: {}}, []
+        while ready:
+            cand = []
+            for i in ready:
+                bk = ops[i]["bank"]
+                for e in ("VS" if ops[i]["free"] else eng[i]):
+                    if (i, e) not in base:
+                        t = 0.0
+                        for j, k in pred[i].items():
+                            if k == -1 or (k == 0 and eng[j] == e):
+                                t = max(t, start[j])
+                            else:
+                                t = max(t, done[j] + (LAT if k == 2 or (k == 1 and eng[j] != e) else 0.0))
+                        base[(i, e)] = t
+                    t = base[(i, e)] if e == "R" else max(base[(i, e)], free[e])
+                    if bk is not None:
+                        t = max([t] + [done[j] + LAT for x, j in users[bk].items() if x != e])
+                    cand.append((t + (vpen[i] if ops[i]["free"] and e == "V" else 0.0), -prio[i], i, e, t))
+            best = min(cand)
+            e = best[3]
             if e != "R":
-                busy[e].insert(pos, (t, t + o["c"]))
-            st[i] = t
-            en[i] = t + o["c"] + (0.0 if back else o["lat"])
-            for k in after[i]:
-                cnt[k] -= 1
-                if cnt[k] == 0:
-                    rdy.append(k)
-        return st, en
+                lim = best[0] + WIN + min(PAR["WIN2"], cost[best[2]] * PAR["WINF"])
+                best = min([c for c in cand if c[3] == e and c[0] <= (lim if cost[c[2]] < PAR["SMALL"] else best[0] + WIN)], key=lambda c: c[1])
+            i, t = best[2], best[4]
+            eng[i] = e
+            ready.remove(i)
+            order.append(i)
+            bk = ops[i]["bank"]
+            if bk is not None:
+                for j in users[bk].values():
+                    pred[i][j] = max(pred[i].get(j, 0), 1)
+                users[bk][e] = i
+            start[i] = t
+            c = cost[i] + (ops[i]["more"] if e == "S" else 0.0)
+            if e != "R":
+                free[e] = t + c
+            done[i] = t + c + lat[i]
+            if nb[i]:
+                free["D"] = max(free["D"], t + lat[i] / 2) + nb[i] / BW
+                done[i] = free["D"] + lat[i] / 2
+            for k in succ[i]:
+                left[k] -= 1
+                if left[k] == 0:
+                    ready.append(k)
+        hard = [[j for j, k in pred[i].items() if k == 2 or (k == 1 and eng[j] != eng[i]) or eng[i] == "R"] for i in range(nops)]
+        return order, hard, eng
 
-    def score(order):
+    def score(order, hard, eng):
         tot = 0.0
-        for gf, sf, pf, df, lf in ((1, 1, 1, 1, 1), (0.67, 0.5, 1, 0.7, 1), (1.33, 1.5, 1, 1, 1), (1, 1, 1, 0.6, 2), (1, 1, 0.8, 0.6, 0.5)):
-            dn, fr = [0.0] * nops, {}
+        for cf, gf, sf, df, lf in PAR["VARY"]:
+            dn, fr = [0.0] * nops, {e: 0.0 for e in "VSPGQRD"}
             for i in order:
-                o = ops[i]
-                t = fr.get(o["e"], 0.0) if o["e"] != "R" else 0.0
-                for j in pred[i]:
-                    x = gap(i, j, o["e"])
-                    if x >= 0:
-                        t = max(t, dn[j] + x * lf)
-                c = o["c"] * (gf if o["kind"] == "g" else sf if o["kind"] == "s" else pf if o["e"] == "P" else 1.0)
-                fr[o["e"]] = t + c
-                dn[i] = t + c + o["lat"] * df
-            tot += max(dn)
-        return tot
+                e = eng[i]
+                t = fr[e] if e != "R" else 0.0
+                for j in hard[i]:
+                    if dn[j] + LAT * lf > t:
+                        t = dn[j] + LAT * lf
+                kind = ops[i]["kind"]
+                t += (cost[i] + (ops[i]["more"] if e == "S" else 0.0)) * cf * (gf if kind == "g" else sf if kind == "s" else 1.0)
+                fr[e] = t
+                if nb[i]:
+                    fr["D"] = max(fr["D"], t + lat[i] * df / 2) + nb[i] / BW * df
+                    t = fr["D"] + lat[i] * df / 2
+                dn[i] = t
+            tot += max(dn) / cf
+        return tot / len(PAR["VARY"])
 
+    tags = {}
+    for i, o in enumerate(ops):
+        tags.setdefault(o["tag"] + o["e"], []).append(i)
+    tags = [tags[x] for x in sorted(tags)]
+    either = [i for i in range(nops) if ops[i]["free"]]
+    lean, vpen = [0.0] * nops, [PAR["VPEN"] if c > 350 else PAR["VP0"] for c in cost]
     keep = None
-    for _it in range(ROUNDS):
-        st, en = place([-d for d in done], True)
-        start, done = place([-x for x in en], False)
-        order = sorted(range(nops), key=lambda i: (start[i], i))
-        sc = score(order)
-        if keep is None or sc < keep[0]:
-            keep = (sc, order, [{j: hard(i, j, ops[i]["e"]) for j in pred[i]} for i in range(nops)], start, done, [o["e"] for o in ops])
-    for i in range(nops):
-        ops[i]["e"] = keep[5][i]
-    return keep[1:5]
+    for _it in range(PAR["ROUNDS"]):
+        l2, v2 = list(lean), list(vpen)
+        if keep is not None:
+            for _k in range(1 + int(2 * rnd())):
+                x = rnd()
+                if x < 0.4:
+                    d = PAR["JT"] * (rnd() - 0.5)
+                    for i in tags[int(rnd() * len(tags))]:
+                        l2[i] += d
+                elif x < 0.6:
+                    l2[int(rnd() * nops)] += PAR["JT"] * (rnd() - 0.5)
+                else:
+                    i = either[int(rnd() * len(either))]
+                    v2[i] = PAR["JG"] * rnd() * (1.0 if cost[i] > 350 else 0.2)
+        res = greedy(l2, v2)
+        sc = score(*res)
+        if keep is None or sc <= now + PAR["TOL"] * rnd() * (1 - _it / PAR["ROUNDS"]):
+            now, lean, vpen = sc, l2, v2
+        if keep is None or sc <= keep[0]:
+            keep = (sc,) + res
+    return keep
+
+
+PLANS = {}
 
 
 def rank_program(g, core, T, topo):
@@ -603,12 +681,15 @@ def rank_program(g, core, T, topo):
     if rank is None:
         return
     ops, nloc = build(g, T, topo, rank)
-    order, pred, start, done = plan(ops)
+    if "plan" not in PLANS:
+        PLANS["plan"] = plan(ops)
+    _sc, order, hard, engine = PLANS["plan"]
     queues = {"V": g.vector, "S": g.scalar, "P": g.tensor, "Q": g.sync, "G": g}
     need = set()
     for i in range(len(ops)):
-        for j, hard in pred[i].items():
-            if hard and ops[j]["sem"] is None:
+        ops[i]["e"] = engine[i]
+        for j in hard[i]:
+            if ops[j]["sem"] is None:
                 need.add(j)
     count = {e: 0 for e in queues}
     mark = {}
@@ -619,8 +700,8 @@ def rank_program(g, core, T, topo):
         if e == "R":
             continue
         waits = {}
-        for j, hard in pred[i].items():
-            if not hard:
+        for j in hard[i]:
+            if ops[j]["sem"] == "none":
                 continue
             if ops[j]["sem"] is None:
                 nm, c = "s" + ops[j]["e"], mark[j]

from concourse.bass import DstId, RemoteDMATransfer
from concourse.mybir import AluOpType, AxisListType, ActivationFunctionType

W, K, ST = 4096, 192, 4
NB = 2
LB = K // NB
TWW = W + K
DLW = 204
BK = (0, 1, 0)
PAR = dict(CUT=((48, 48), (48, 48), (32, 32, 32), (48, 48)),
           PLAIN=3,
           CHAIN=(2, 3, 4),
           SPLIT=((0, 0), (1, 1)),
           WHO={},
           TOL=300.0, VP0=30.0, WB=2000.0, WIN2=0.0, WINF=0.4, SMALL=300.0, HALF=(1, 3), KS=(0, 1, 2, 3, 4, 5), WAV=12, WAB=8000.0,
           ORDER=((0, 0), (0, 1), (1, 0), (0, 2), (1, 1), (1, 2)),
           ROUNDS=2000, VPEN=400.0, WIN=30.0, SEED=1, JG=1500.0, JT=2000.0,
           VARY=((1, 1, 1, 1, 1), (0.9, 0.7, 0.5, 1.2, 1), (1.25, 1.3, 1.4, 1, 1), (1, 0.7, 1.3, 1, 2.2), (1, 1.2, 1, 1.7, 1)),
           CY=0.87, PC=0.435, GC=1.56, SCC=3.8, LAT=110.0, FIX=35.0, DL=1200.0, RL=1500.0, BW=330.0)
DELTAS = [(s, d) for s in range(1, ST + 1) for d in range(1, ST + 2 - s)]


def sb(n, dtype):
    return ("sbuf", [128, n], dtype)


SCRATCH = {}
for _n, _c in dict(tw=W, tws=512, wv=4 * W, g0=16 * K, g1=16 * K, g2=16 * K, ff=16 * K, kk=16 * K, zb=512, mk=512, ee=12 * 194, zd=144, idb=128,
                   n256=128, bda=2048, bdb=128, wk=16, ws=128, c15=256, one=512, eps=128, c3=ST, c49=512,
                   zo=144, zl=144, bdl=256, idn=128, ide=128, idl=128, sd=384).items():
    SCRATCH[_n] = sb(_c, "bfloat16")
for _n, _c in dict(wb=TWW, wc=TWW, lf=1024, tf=1024, tl=4096, yo=K, zr=512, rm=512, wf=12, sc=12 * 194, dd=194, oo=16 * 12, cc=32,
                   ia=144, ig=128, it=128, ik=8, ij=12, ma=16, t1=128, t2=256, t3=128, t5=128, t6=144, pr=128, t4=64, rs=256).items():
    SCRATCH[_n] = sb(_c, "float32")
for _n, _c in dict(wa=W, lfi=1024, imgi=K, yi=K, ya=K, owi=K, ti=512, ci=4).items():
    SCRATCH[_n] = sb(_c, "int32")
for _n, _c in dict(dl=DLW * len(DELTAS), sv=DLW * ST, uu=K, wo=12).items():
    SCRATCH[_n] = sb(_c, "uint16")
for _n, _c in dict(bc=K, mb=K, e0=K, e1=K, tc=512, th=16 * K, mc=12, wr=K, kr=194, wt=128).items():
    SCRATCH[_n] = sb(_c, "float16")
for _n in ["pf%d" % _i for _i in range(6)] + ["px0", "px1"]:
    SCRATCH[_n] = ("psum", [128, 512], "float32")

SEMAPHORES = (["sV", "sS", "sP", "sG", "rloc", "rvw"] + ["rt%d" % k for k in range(1, 5)] + ["rf%d" % k for k in range(1, 5)]
              + ["rd%d%d" % sd for sd in DELTAS] + ["q%d" % i for i in range(36)])


def build(g, T, topo, rank):
    A = AluOpType
    F = ActivationFunctionType
    V, S, P, Q = g.vector, g.scalar, g.tensor, g.sync
    PLAIN, CHAIN, CY, PC, GC, SCC = [PAR[x] for x in ("PLAIN", "CHAIN", "CY", "PC", "GC", "SCC")]
    cores = T.cores
    n = len(cores)
    me = cores[rank]
    ops = []
    lead = [0.0]
    tag = [""]
    gathers = {}
    lists = [(s, d) for (s, d) in DELTAS if d == 1 or all(k not in CHAIN for k in range(s + 1, s + d))]

    def op(eng, fn, r, w, cost, lat=0.0, sem=None, cnt=0, after=None, bias=0.0, kind="", nbytes=0, more=0.0):
        bank = None
        if eng == "Y":
            eng, fn = "V", fn[0]
        for x in w:
            if x[:2] in ("#x", "#w"):
                bank = int(x[2])
        ops.append({"bank": bank, "free": eng == "X", "e": eng, "fn": fn, "r": list(r), "w": list(w), "c": cost, "lat": lat, "sem": sem,
                    "cnt": cnt, "after": after, "behind": None, "more": more, "bytes": nbytes, "bias": bias + lead[0], "kind": kind, "tag": tag[0]})
        return len(ops) - 1

    def vc(nel, f=1.0):
        return max(64.0, nel * f) * CY + PAR["FIX"]

    def ts(out, in0, s1, s2, o0, o1, r, w, nel, f=1.0):
        if o1 is None:
            return op("V", lambda: V.tensor_scalar(out, in0, s1, None, o0), r, w, vc(nel, f))
        return op("V", lambda: V.tensor_scalar(out, in0, s1, s2, o0, o1), r, w, vc(nel, f))

    def tt(out, a, b, o, r, w, nel, f=2.0):
        return op("V", lambda: V.tensor_tensor(out, a, b, o), r, w, vc(nel, f))

    def xs(out, in_, scale, bias, r, w, nel, f=1.0, kind=""):
        return op("X", (lambda: V.tensor_scalar(out, in_, scale, bias, A.mult, A.add),
                        lambda: S.activation(out, in_, F.Identity, bias=bias, scale=scale)), r, w, vc(nel, f), more=vc(nel, max(f, 1.0)) - vc(nel, f),
                  kind=kind)

    def act(out, in_, scale, bias, r, w, nel, func=F.Identity):
        return op("S", lambda: S.activation(out, in_, func, bias=bias, scale=scale), r, w, vc(nel))

    def cp(out, in_, r, w, nel, f=1.0):
        return op("V", lambda: V.tensor_copy(out, in_), r, w, vc(nel, f))

    def ms(ap, val, w, nel):
        return op("V", lambda: V.memset(ap, val), [], w, vc(nel))

    def scan(out, d0, d1, init, o0, o1, r, w, nel):
        return op("V", lambda: V.tensor_tensor_scan(out, d0, d1, init, o0, o1), r, w, vc(nel))

    def io(out, pat, base, cm, w, nel, isint=False):
        if isint:
            return op("G", lambda: g.iota(out, pat, base, cm), [], w, 130 + 2 * nel * CY)
        return op("G", lambda: g.iota(out, pat, base, cm, allow_small_or_imprecise_dtypes=True), [], w, 130 + 2 * nel * CY)

    def mm(lst, r, w):
        def fn():
            last = None
            for (o, l, x, a, b, _c) in lst:
                last = P.matmul(o, l, x, a, b)
            return last
        return op("P", fn, r, w, sum(x[5] for x in lst) * PC)

    ndma = [0]

    def dma(pairs, r, w, nbytes, eng="Q", bias=0.0, after=None):
        sem = "q%d" % ndma[0]
        ndma[0] += 1
        q = Q if eng == "Q" else S

        def fn():
            for (o, i) in pairs:
                q.dma_start(o, i).then_inc(T.sem[sem], 16)
        return op(eng, fn, r, w, 60.0 * len(pairs), lat=PAR["DL"], nbytes=nbytes, sem=sem, cnt=16 * len(pairs), bias=bias, after=after)

    rloc = [0]
    first = [True]

    def remote(trs, r, nbytes, bias=0.0, local="rloc"):
        lst = []
        for (src, dsts, lo, k, sem) in trs:
            to = [cores[(rank + d) % n] for d, _x in dsts]
            m = 0
            for e in topo.engines(me, to[0])[lo:lo + k]:
                m |= 1 << e
            lst.append(RemoteDMATransfer(dst_ids=[DstId(rid=topo.addr(c)[0], pnc=topo.addr(c)[1]) for c in to], dma_engine_mask=m,
                                         remote_sem=T.sem[sem], srcs=[src], dsts=[x for _d, x in dsts]))
            if local == "rloc":
                rloc[0] += k
        if first[0]:
            first[0] = False
            op("G", lambda: None, r, ["late"], 1700.0, sem="none", bias=bias)
            r = r + ["late"]
        return op("G", lambda: g.remote_dma_fused(lst, local_sem=T.sem[local]), r, [], 300.0, lat=PAR["RL"], nbytes=nbytes * 1.3, sem="none", bias=bias)

    def recv(sem, cnt, w, after):
        return op("R", None, [], w, 0.0, sem=sem, cnt=cnt, after=after)

    cc, oo = T.cc, T.oo
    pcol, gcol, tcol, wcol, c12, nlc, p16, s1c, s2c, s3c = [cc[:, i:i + 1] for i in range(10)]
    O = {}
    for i, nm in enumerate(["mc", "x", "ko", "win", "a", "b", "dm", "j", "jo", "d1", "d2", "c", "b2"]):
        O[nm] = oo[:, 12 * i:12 * i + 12]
    PF = [T["pf%d" % i] for i in range(6)]
    PX = [T.px0, T.px1]
    WN = ["wa", "wb", "wc", "wb", "wc"]
    WT = [T[x] for x in WN]
    EE = [T.e0, T.e1]
    GG = [T.g0, T.g1, T.g2]
    ne = len(topo.engines(me, cores[(rank + 1) % n]))

    sl = slice(512 * rank, 512 * rank + 512)
    d0 = dma([(T.ti[0:8, :], T.turn[:, sl])], [], ["ti"], 16384, bias=9000)
    d0 = dma([(T.tws[:, :], T.twist[:, sl])], [], ["tws"], 131072, bias=9000, after=d0)
    d0 = dma([(T.imgi[:, :], T.img[:, :])], [], ["imgi"], 98304, bias=3000, after=d0)
    d1 = dma([(T.tw[:, :], T.twist[:, :])], [], ["tw"], 1048576, bias=8000, after=d0)
    lead[0] = PAR["WAB"]
    nv = PAR["WAV"]
    ms(T.rs[:, :], 0.0, ["rs"], 256)
    for h in range(nv):
        o_ = T.wa[:, 256 * h:256 * h + 256]
        op("X", (lambda o_=o_: V.memset(o_, 0), lambda o_=o_: S.activation(o_, T.rs[:, :], F.Identity)), ["rs"], ["wa%d" % h], vc(256))
    fill = io(T.wa[:, 256 * nv:W], [[0, W - 256 * nv]], 0, 0, ["wag"], W - 256 * nv, True)
    d2 = dma([(T.wa[4 * c::16, :], T.ent[:, W * c:W * c + W]) for c in range(3)] + [(T.wa[12::16, :], T.elen[:, :])],
             ["wa%d" % h for h in range(nv)] + ["wag"], ["wa"], 524288, after=d1)
    lead[0] = 0.0
    lead[0] = 30000.0
    ms(T.owi[:, :], 0, ["owi"], K)
    dma([(T.owi[4 * c::16, :], T.own[:, K * c:K * c + K]) for c in range(3)] + [(T.owi[12::16, :], T.olen[:, :])],
        [], ["owi"], 30000, after=d1)

    lead[0] = 9000.0
    io(T.ci[:, 0:1], [[0, 1]], 0, 1, ["ci0"], 1, True)
    io(T.ig[:, :], [[16, 8], [0, 16]], 0, 0, ["ig"], 128)
    io(T.it[:, :], [[0, 8], [1, 16]], 0, 0, ["it"], 128)
    ops[fill]["after"] = io(T.ia[:, :], [[1, 144]], -15, 0, ["ia"], 144)
    ts(T.ci[:, 1:2], T.ci[:, 0:1], 112, None, A.bitwise_and, None, ["ci0"], ["ci1"], 1)
    ts(T.ci[:, 2:3], T.ci[:, 0:1], 15, None, A.bitwise_and, None, ["ci0"], ["ci2"], 1)
    cp(cc[:, 0:3], T.ci[:, 0:3], ["ci0", "ci1", "ci2"], ["c012"], 3)
    ts(T.t1[:, :], T.it[:, :], 13.0, 0.5, A.is_lt, A.mult, ["it"], ["t1"], 128)
    ts(T.t2[:, 0:128], T.it[:, :], 0.0, None, A.is_equal, None, ["it"], ["t2"], 128)
    scan(T.pr[:, :], T.t1[:, :], T.t2[:, 0:128], 0.0, A.mult, A.add, ["t1", "t2"], ["pr"], 128)
    act(c12, tcol, -1.0, 12.0, ["c012"], ["c12"], 1)
    ts(T.t4[:, 0:16], T.it[:, 0:16], c12, 8.0, A.is_equal, A.mult, ["it", "c12"], ["t4a"], 16)
    tt(T.t4[:, 32:48], T.t4[:, 0:16], T.pr[:, 0:16], A.mult, ["t4a", "pr"], ["t4c"], 16)
    op("V", lambda: V.tensor_reduce(wcol, T.t4[:, 32:48], AxisListType.X, A.add), ["t4c"], ["wcol"], vc(16))
    ts(T.bdb[:, :], T.ig[:, :], gcol, None, A.is_equal, None, ["ig", "c012"], ["bdb"], 128)
    tt(T.t2[:, 128:256], T.bdb[:, :], T.pr[:, :], A.mult, ["bdb", "pr"], ["t2b"], 128)
    act(T.ws[:, :], T.t2[:, 128:256], wcol, 0.0, ["t2b", "wcol"], ["ws"], 128)
    act(p16, pcol, 16.0, 0.0, ["c012"], ["p16"], 1)
    ts(T.t3[0:8, :], T.ig[0:8, :], cc[0:8, 6:7], None, A.is_equal, None, ["ig", "p16"], ["t3"], 128)
    tt(T.wt[0:8, :], T.t3[0:8, :], T.pr[0:8, :], A.mult, ["t3", "pr"], ["wt"], 128)
    act(T.eps[0:1, :], T.pr[0:1, :], 2.0 ** -10, 0.0, ["pr"], ["eps"], 128)
    ms(T.one[0:2, :], 1.0, ["one"], 256)
    act(T.t5[:, :], T.ia[:, 15:143], -1.0, pcol, ["ia", "c012"], ["t5"], 128, F.Abs)
    act(T.idb[:, :], T.t5[:, :], -1.0, 1.0, ["t5"], ["idb"], 128, F.Relu)
    act(T.n256[:, :], T.idb[:, :], -256.0, 0.0, ["idb"], ["n256"], 128)
    ma = [T.ma[:, a:a + 1] for a in range(16)]
    lead[0] = 20000.0
    ts(T.ma[:, :], T.it[:, 0:16], tcol, None, A.is_equal, None, ["it", "c012"], ["ma"], 16)
    lead[0] = 0.0
    act(T.c15[0:1, 0:16], T.it[0:1, 0:16], -1.0, 15.0, ["it"], ["c15"], 16)
    act(T.c15[0:1, 16:32], T.it[0:1, 0:16], 0.0, -65536.0, ["it"], ["c15"], 16)
    for k in (32, 64, 128):
        act(T.c15[0:1, k:2 * k], T.c15[0:1, 0:k], 1.0, 0.0, [], ["c15"], k)
    act(T.ij[:, 0:8], T.ig[:, 0::16], 1.0, 0.0, ["ig"], ["ija"], 8)
    act(T.ij[:, 8:12], T.ig[:, 0:64:16], 1.0, 128.0, ["ig"], ["ijb"], 4)
    act(T.ik[:, 0:4], T.ig[:, 0::32], 1.0, 0.0, ["ig"], ["ika"], 4)
    act(T.ik[:, 4:8], T.ig[:, 16::32], 1.0, 0.0, ["ig"], ["ikb"], 4)
    act(nlc, ma[12], -1.0, 1.0, ["ma"], ["nlc"], 1)
    act(T.ide[:, :], T.idb[:, :], nlc, 0.0, ["idb", "nlc"], ["ide"], 128)
    act(T.idl[:, :], T.idb[:, :], ma[12], 0.0, ["idb", "ma"], ["idl"], 128)
    act(T.t6[:, :], T.ia[:, :], -1.0, gcol, ["ia", "c012"], ["t6"], 144, F.Abs)
    act(T.zo[:, :], T.t6[:, :], -1.0, 1.0, ["t6"], ["zo"], 144, F.Relu)
    for s in range(1, ST + 1):
        act(cc[:, 16 + s:17 + s], ma[12], 3.0 * (s - 1), 2048.0, ["ma"], ["svc%d" % s], 1)
    act(T.c3[0:1, :], T.it[0:1, 0:ST], 3.0, 0.0, ["it"], ["c3"], ST)
    act(T.zl[:, :], T.zo[:, :], ma[12], 0.0, ["zo", "ma"], ["zl"], 144)
    act(T.bdl[:, 0:128], T.bdb[:, :], ma[12], 0.0, ["bdb", "ma"], ["bdl"], 128)
    act(T.bdl[:, 128:256], T.bdl[:, 0:128], -1.0, 0.0, ["bdl"], ["bdn"], 128)
    act(T.idn[:, :], T.idb[:, :], -1.0, 0.0, ["idb"], ["idn"], 128)
    act(T.zd[:, :], T.zo[:, :], wcol, 0.0, ["zo", "wcol"], ["zd"], 144)
    for q, (c, lo, hi) in enumerate([(s1c, ma[0], ma[4]), (s2c, ma[4], ma[8]), (s3c, ma[8], 0.0)]):
        act(c, lo, -1.0, hi, ["ma"], ["sc%dc" % q], 1)
        act(T.sd[:, 128 * q:128 * q + 128], T.bdb[:, :], c, 0.0, ["bdb", "sc%dc" % q], ["sd%d" % q], 128)
    for a in range(16):
        act(T.bda[:, 128 * a:128 * a + 128], T.bdb[:, :], ma[a], 0.0, ["bdb", "ma"], ["bda%d" % a], 128)
    BDA = ["bda%d" % a for a in range(16)]
    ts(T.wk[:, 0:8], T.ik[:, :], gcol, 16.0, A.is_equal, A.mult, ["ika", "ikb", "c012"], ["wk"], 8)
    act(T.wk[:, 8:16], T.wk[:, 0:8], -1.0, 0.0, ["wk"], ["wkn"], 8)
    ms(T.rs[:, 0::32], -2.0 ** 20, ["rs"], 8)
    act(cc[0:2, 10:11], cc[0:2, 0:1], 127.5 - 49152.0, 49152.0, ["c012"], ["c49c"], 1)
    act(T.c49[0:2, :], T.one[0:2, :], cc[0:2, 10:11], 0.0, ["one", "c49c"], ["c49"], 512)
    ts(T.kr[:, 0:1], pcol, 0.0, None, A.mult, None, ["c012"], ["kr0"], 1)
    ms(T.ee[:, 192::194], -193.0 / 256, ["eec"], 12)
    act(O["j"], T.ij[:, :], 1.0, tcol, ["ija", "ijb", "c012"], ["j"], 12)
    act(O["jo"], O["j"], 1.0 / 256, -0.75, ["j"], ["jo"], 12)
    act(O["d1"], O["j"], 1.0, 2048.0, ["j"], ["d1"], 12)
    act(O["d2"], O["j"], 1.0, 4096.0, ["j"], ["d2"], 12)

    lead[0] = 9000.0
    xs(T.tc[0:8, :], T.ti[0:8, :], -1.0, 2048.0, ["ti"], ["tc"], 512)
    c0 = (512 * rank + 2048) % W
    mine = T.wv[:, c0:c0 + 512]
    for h in range(2):
        hs = slice(256 * h, 256 * h + 256)
        Z, Y = PF[h][:, 0:256], PF[2 + h][:, 0:256]
        mm([(Z, T.eps[0:1, :], T.one[0:1, hs], True, False, 256), (Z, T.ws[:, :], T.tws[:, hs], False, False, 256),
            (Z, T.wt[0:8, :], T.tc[0:8, hs], False, True, 256)], ["ws", "tws", "wt", "tc", "eps", "one"], ["#f%d" % h])
        ts(T.zr[:, hs], Z, 1.5 * 2 ** 23, 1.5 * 2 ** 23, A.add, A.subtract, [], ["#f%d" % h, "zr%d" % h], 256)
        tt(T.zb[:, hs], T.zr[:, hs], Z, A.is_gt, ["zr%d" % h], ["#f%d" % h, "zb%d" % h], 256, 1.0)
        mm([(Y, T.idb[:, :], T.tws[:, hs], True, False, 256), (Y, T.n256[:, :], T.zb[:, hs], False, True, 256)],
           ["idb", "tws", "n256", "zb%d" % h], ["#f%d" % (2 + h)])
        made = act(mine[:, hs], Y, 1.0, 0.0, [], ["#f%d" % (2 + h), "wvm%d" % h], 256)
    o = remote([(mine, [(d, mine) for d in range(1, n)], 0, ne, "rvw")], ["wvm0", "wvm1"], 7 * 131072, bias=5000)
    recv("rvw", ne * (n - 1), ["wvr"], o)
    lead[0] = 0.0

    dma([(T.lfi[:, 256 * c:256 * c + 256], T.ent[:, W * c:W * c + W]) for c in range(3)] + [(T.lfi[:, 768:1024], T.elen[:, :])],
        ["wa"], ["lfi"], 524288)
    for h in range(2):
        xs(T.lf[:, 512 * h:512 * h + 512], T.lfi[:, 512 * h:512 * h + 512], 1.0, 0.0, ["lfi"], ["lf%d" % h], 512)
    for nm in ("wb", "wc"):
        for h in range(8):
            i = io(T[nm][:, 536 * h:536 * h + 536], [[0, 536]], 0, 0, [nm], 536)
            ops[i]["after"] = o
            o = i

    def unfold(k, extra):
        c0 = 1024 * (k - 1)
        dma([(WT[k][4 * c::16, 0:W], T.tl[:, c0 + 256 * c:c0 + 256 * c + 256]) for c in range(4)], ["tl%d" % k] + extra, [WN[k], "un%d" % k], 524288)

    def send_table(k, extra):
        o = remote([(T.lf[:, :], [(k, T.tl[:, 1024 * (k - 1):1024 * k])], 0, ne, "rt%d" % k)], ["lf0", "lf1"] + extra, 524288)
        recv("rt%d" % k, ne, ["tl%d" % k], o)

    def pass_table(k):
        dma([(T.tf[:, 256 * c:256 * c + 256], WT[k - 1][4 * c::16, 0:W]) for c in range(4)], [WN[k - 1]], ["tf"], 524288)
        o = remote([(T.tf[:, :], [(1, T.tl[:, 1024 * (k - 1):1024 * k])], 0, ne, "rt%d" % k)], ["tf"], 524288, local="rf%d" % k)
        recv("rt%d" % k, ne, ["tl%d" % k], o)
        recv("rf%d" % k, ne, ["tf"], o)

    def copy_window(c, extra):
        dma([(T.wv[:, W * c:W * c + W], T.wv[:, 0:W])], ["wvm0", "wvm1", "wvr"] + extra, ["wv%d" % c], 1048576)

    send_table(1, ["wvr"])
    copy_window(1, [])
    copy_window(2, ["wv1"])
    unfold(1, ["wv1"])
    copy_window(3, ["wv2"])
    last = "wv3"
    for k in range(2, ST + 1):
        if k not in CHAIN:
            send_table(k, [last])
            last = "tl%d" % k
            if k == 2:
                unfold(2, [])
                last = "un2"

    def scatter(s, d):
        if (s, d) not in lists:
            return
        tag[0] = "s%d%d" % (s, d)
        k = d + s - 1
        i = DELTAS.index((s, d))
        win = WT[k]
        op("V", lambda: V.tensor_copy(win[:, 0:TWW].indirect(T.dl[:, DLW * i + K:DLW * i + K + 12]), T.dl[:, DLW * i:DLW * i + K]),
           ["dl%d%d" % (s, d)], [WN[k]], 50 + K * SCC * CY, kind="s")

    xs(EE[0][:, :], T.owi[:, :], 1.0, -2048.0, ["owi"], ["e0_0", "e0_1"], K)
    mm([(PX[1][:, 256:268], T.zl[:, 15 - a:143 - a], EE[0][:, a::16], a == 0, a == 15, 64) for a in range(16)],
       ["zl", "e0_0", "e0_1"], ["#w1"])
    xs(T.mc[:, :], PX[1][:, 256:268], 1.0, 0.0, [], ["#w1", "mc"], 12)
    lead[0] = 20000.0
    xs(T.uu[:, :], T.imgi[:, :], 1.0, 0.0, ["imgi"], ["u_%d" % k for k in range(K // 16)], K)
    lead[0] = 0.0
    xs(T.bc[:, :], T.imgi[:, :], 1.0, -2048.0, ["imgi"], ["bc0", "bc1"], K)

    def pieces(nm, l0, l1):
        return [nm + "_%d" % k for k in range(l0 // 16, l1 // 16)]

    def gather(b, win, wr, out, nm, key):
        l0 = LB * b
        for gl in PAR["CUT"][key[2]]:
            o_, i_ = out[:, 16 * l0:16 * (l0 + gl)], win.indirect(T.uu[:, l0:l0 + gl])
            if key[0]:
                fns = (lambda o_=o_, i_=i_: V.tensor_copy(o_, i_), lambda o_=o_, i_=i_: S.activation(o_, i_, F.Identity))
            else:
                fns = (lambda o_=o_, i_=i_: V.tensor_scalar(o_, i_, -127.5, None, A.add),
                       lambda o_=o_, i_=i_: S.activation(o_, i_, F.Identity, bias=-127.5))
            who = PAR["WHO"].get((key, len(gathers.get(key, []))), "X")
            i = op(who, fns if who == "X" else fns[who == "S"], wr + pieces("u", l0, l0 + gl), pieces(nm, l0, l0 + gl),
                   60 + 16 * gl * GC * CY, kind="g", after=made if who == "S" and not key[0] else None)
            gathers.setdefault(key, []).append(i)
            l0 += gl

    tag[0] = "f0"
    for b in range(NB):
        gather(b, T.tw[:, 0:W], ["tw"], T.ff, "ff", (0, b, 3))
    rounder = {}
    HALF = PAR["HALF"]

    def begin(s, ch):
        src, r = (T.th, ["th%d" % ch]) if s - 1 in HALF else (T.ff, pieces("ff", 32 * ch, 32 * ch + 32))
        rows = 2 if s == ST else 1

        def fn():
            lift = s == ST or ops[rounder[(s, ch)]]["e"] == "S"
            if lift:
                P.matmul(PF[ch][:, :], T.one[0:rows, 0:128], T.c49[0:rows, :], True, False)
            return P.matmul(PF[ch][:, :], T.idb[:, :], src[:, 512 * ch:512 * ch + 512], not lift, False)
        op("P", fn, ["one", "c49", "idb"] + r, ["#f%d" % ch], (1024 if s == ST or ch in PAR["KS"] else 512) * PC)

    def to_list(b, add, plain, l0=0, l1=LB):
        ls = slice(LB * b + l0, LB * b + l1)
        x = pieces("#x%d" % b, l0, l1)
        u, yi, ya = [pieces(nm, LB * b + l0, LB * b + l1) for nm in ("u", "yi", "ya")]
        if plain:
            xs(T.uu[:, ls], PX[b][:, l0:l1], 1.0, add, [], x + u, l1 - l0)
        else:
            xs(T.yi[:, ls], PX[b][:, l0:l1], 1.0, add, [], x + yi, l1 - l0)
            ts(T.ya[:, ls], T.yi[:, ls], W - 1, None, A.bitwise_and, None, yi, ya, l1 - l0)
            xs(T.uu[:, ls], T.ya[:, ls], 1.0, 0.0, ya, u, l1 - l0)

    def choose(s, b):
        tag[0] = "c%d%d" % (s, b)
        ls = slice(LB * b, LB * b + LB)
        x = pieces("#x%d" % b, 0, LB)
        X = PX[b]
        c0 = 16 * LB * b
        if s - 1 in HALF:
            parts = [(T.th, T.wk[:, 0:8]), (T.kk, T.wk[:, 8:16])]
            fr = [nm + "%d" % ch for ch in range(3 * b, 3 * b + 3) for nm in ("th", "kk")]
        else:
            parts, fr = [(T.ff, T.wk[:, 0:8])], pieces("ff", LB * b, LB * b + LB)
        mm([(X[0:LB, 0:256], T.one[0:1, 0:LB], T.c15[0:1, :], True, False, 256)]
           + [(X[0:LB, i:256:32], f_[:, c0 + i:c0 + 16 * LB:16], w_, False, i == 15 and f_ is parts[-1][0], 64)
              for (f_, w_) in parts for i in range(16)], ["one", "c15", "wk", "wkn"] + fr, x)
        scan(T.rm[0:LB, 256 * b:256 * b + 256], T.rs[0:LB, :], X[0:LB, 0:256], -2.0 ** 20, A.add, A.max, ["rs"], x + ["rm%d" % b], 256)
        tt(T.mk[0:LB, 256 * b:256 * b + 240], X[0:LB, 0:240], T.rm[0:LB, 256 * b + 16:256 * b + 256], A.is_equal,
           ["rm%d" % b], x + ["mk%d" % b], 240, 1.0)
        mm([(X[:, 0:LB], T.mk[0:LB, 256 * b:256 * b + 128], T.idb[0:LB, 0:LB], True, False, LB),
            (X[:, 0:LB], T.mk[0:LB, 256 * b + 112:256 * b + 240], T.idb[0:LB, 0:LB], False, True, LB)], ["mk%d" % b, "idb"], x)
        tt(T.mb[:, ls], X[:, 0:LB], T.bc[:, ls], A.mult, ["bc%d" % b], x + ["mb%d" % b], LB, 1.0)
        nc = LB // 16
        mm([(X[:, 0:nc], T.zo[:, 15 - a:143 - a], T.mb[:, LB * b + a:LB * b + LB:16], a == 0, a == 15, 64) for a in range(16)],
           ["zo", "mb%d" % b], x)
        os_ = slice(nc * b, nc * b + nc)
        xs(T.wo[:, os_], X[:, 0:nc], 1.0, 2048.0, [], x + ["wo%d" % b], nc)
        E = EE[s % 2]
        xs(E[:, ls], WT[s - 1][:, 0:W].indirect(T.wo[:, os_]), 1.0, -2048.0, ["wo%d" % b, WN[s - 1]], ["e%d_%d" % (s % 2, b)], LB + 12, GC, "g")
        mm([(X[:, 0:LB], T.idb[:, :], T.bc[:, ls], True, False, LB), (X[:, 0:LB], T.bda[:, 0:128], E[:, ls], False, True, LB)],
           ["idb", "bc%d" % b, "bda0", "e%d_%d" % (s % 2, b)], x)
        to_list(b, 6144.0, 3 * (s - 1) >= PLAIN)

    def winners(s):
        tag[0] = "w%d" % s
        lead[0] = PAR["WB"]
        E, Ep = EE[s % 2], EE[(s - 1) % 2]
        es, ep = [["e%d_%d" % (x % 2, b) for b in range(NB)] for x in (s, s - 1)]
        X, xw = PX[BK[0]][:, 256:512], "#w%d" % BK[0]
        if s == 1:
            mm([(X[:, 0:K], T.bdl[:, 0:128], Ep[:, :], True, True, K)], ["bdl"] + ep, [xw])
        else:
            mm([(X[:, a:192:16], T.bda[:, 128 * a:128 * a + 128], T.mc[:, :], True, True, 64) for a in range(16)], ["mc"] + BDA, [xw])
        xs(T.kr[:, 1:193], X[:, 0:K], 1.0, 0.0, [], [xw, "kr"], K)
        mm([(X[:, 0:K], T.ide[:, :], Ep[:, :], True, False, K), (X[:, 0:K], T.idl[:, :], T.kr[:, 1:193], False, True, K)],
           ["ide", "idl", "kr"] + ep, [xw])
        xs(T.sv[:, DLW * (s - 1):DLW * (s - 1) + K], X[:, 0:K], 1.0, cc[:, 16 + s:17 + s], ["svc%d" % s], [xw, "sv%da" % s], K)
        mm([(X[:, 0:K], T.bdb[:, :], T.mb[:, :], True, True, K)], ["bdb", "mb0", "mb1"], [xw])
        xs(T.wr[:, :], X[:, 0:K], 1.0, 0.0, [], [xw, "wr"], K)
        xs(T.wf[:, :], T.wo[:, :], 1.0, -2048.0, ["wo0", "wo1"], ["wf"], 12)
        X, xw = PX[BK[1]][:, 256:512], "#w%d" % BK[1]
        mm([(X[:, 0:193], T.idb[:, :], T.kr[:, 0:193], True, False, 193), (X[:, 0:K], T.idn[:, :], T.kr[:, 1:193], False, False, K)]
           + ([(X[:, 192:193], T.one[0:1, 0:128], T.c3[0:1, s - 1:s], False, False, 64)] if s > 1 else [])
           + [(X[:, 0:K], T.bdl[:, 0:128], E[:, :], False, False, K), (X[:, 1:193], T.bdl[:, 128:256], E[:, :], False, True, K)],
           ["idb", "idn", "kr", "kr0", "one", "c3", "bdl", "bdn"] + es, [xw])
        xs(T.dd[:, 0:193], X[:, 0:193], 1.0, -1.0 / 256, [], [xw, "dd"], 193)
        for c in range(12):
            ts(T.ee[:, 194 * c:194 * c + K], T.wr[:, :], T.wf[:, c:c + 1], 16384.0, A.not_equal, A.mult, ["wr", "wf"], ["ee%d" % c], K, 0.5)
        for c in range(12):
            scan(T.sc[:, 194 * c:194 * c + 193], T.dd[:, 0:193], T.ee[:, 194 * c:194 * c + 193], 16384.0, A.add, A.min,
                 ["dd", "ee%d" % c, "eec"], ["sc%d" % c], 193)
        tt(O["a"], T.wf[:, :], O["d1"], A.subtract, ["wf", "d1"], ["a"], 12)
        tt(O["x"], T.sc[:, 192::194], O["jo"], A.subtract, ["jo"] + ["sc%d" % c for c in range(12)], ["x"], 12)
        ts(O["dm"], O["x"], 1.5 * 2 ** 23, 1.5 * 2 ** 23, A.add, A.subtract, ["x"], ["dm"], 12)
        tt(O["win"], O["x"], O["dm"], A.is_equal, ["x", "dm"], ["win"], 12)
        tt(O["b"], O["a"], O["win"], A.mult, ["a", "win"], ["b"], 12)
        tt(O["c"], O["b"], O["d2"], A.add, ["b", "d2"], ["c"], 12)
        xs(T.sv[:, DLW * (s - 1) + K:DLW * (s - 1) + K + 12], O["c"], 1.0, 0.0, ["c"], ["sv%db" % s], 12)
        ds = [d for (s2, d) in lists if s2 == s]
        k = ne // {1: 1, 2: 2, 3: 4, 4: 4}[len(ds)]
        src = T.sv[:, DLW * (s - 1):DLW * s]
        o = remote([(src, [(d, T.dl[:, DLW * DELTAS.index((s, d)):DLW * (DELTAS.index((s, d)) + 1)])], k * j, k, "rd%d%d" % (s, d))
                    for j, d in enumerate(ds)], ["sv%da" % s, "sv%db" % s], 50000 * len(ds))
        for d in ds:
            recv("rd%d%d" % (s, d), k, ["dl%d%d" % (s, d)], o)
        lead[0] = 0.0
        if s < ST:
            tt(O["b2"], O["dm"], O["win"], A.mult, ["dm", "win"], ["b2"], 12)
            tt(T.mc[:, :], T.mc[:, :], O["b2"], A.subtract, ["b2"], ["mc"], 12)

    def letter(s, q, b):
        tag[0] = "l%d%d%d" % (s, q, b)
        ls = slice(LB * b, LB * b + LB)
        G = GG[(q + 1) % 3]
        gn = "g%d" % ((q + 1) % 3)
        if 3 * (s - 1) + q < PLAIN:
            gather(b, T.wv[:, 0:W], ["wvm0", "wvm1", "wvr"], G, gn, (s, b, q))
        else:
            gather(b, T.wv[:, 0:4 * W], ["wvm0", "wvm1", "wvr", "wv1", "wv2", "wv3"], G, gn, (s, b, q))
        X = PX[b]
        for (l0, l1) in ([(0, LB // 2), (LB // 2, LB)] if (b, q) in PAR["SPLIT"] else [(0, LB)]):
            g0, g1 = LB * b + l0, LB * b + l1
            mm([(X[:, l0:l1], T.sd[:, 128 * q:128 * q + 128], EE[s % 2][:, g0:g1], True, False, max(64, l1 - l0))]
               + [(X[:, l0:l1], T.zd[:, 15 - i:143 - i], G[:, 16 * g0 + i:16 * g1:16], False, i == 15, max(64, l1 - l0)) for i in range(16)],
               ["sd%d" % q, "e%d_%d" % (s % 2, b), "zd"] + pieces(gn, g0, g1), pieces("#x%d" % b, l0, l1))
            if q < 2:
                to_list(b, 8192.0, 3 * (s - 1) + q + 1 >= PLAIN, l0, l1)
        for ch in range(3 * b, 3 * b + 3):
            cs = slice(512 * ch, 512 * ch + 512)
            if q == 0 and s not in HALF:
                begin(s, ch)
            mm([(PF[ch][:, :], T.idb[:, :], G[:, cs], q == 0 and s in HALF, q == 2, 512)], ["idb"] + pieces(gn, 32 * ch, 32 * ch + 32), ["#f%d" % ch])
        if q < 2:
            return
        yi, ya = pieces("yi", LB * b, LB * b + LB), pieces("ya", LB * b, LB * b + LB)
        xs(T.yi[:, ls], X[:, 0:LB], 1.0, 8192.0, [], pieces("#x%d" % b, 0, LB) + yi, LB)
        ts(T.ya[:, ls], T.yi[:, ls], W - 1, None, A.bitwise_and, None, yi, ya, LB)
        if s < ST:
            xs(T.bc[:, ls], T.ya[:, ls], 1.0, -2048.0, ya, ["bc%d" % b], LB)
        else:
            xs(T.yo[:, ls], T.ya[:, ls], 1.0, 0.0, ya, ["yo%d" % b], LB)
            dma([(T.yimg[:, ls], T.yo[:, ls])], ["yo%d" % b], [], 50000)
        tag[0] = "k%d%d" % (s, b)
        for ch in range(3 * b, 3 * b + 3):
            cs = slice(512 * ch, 512 * ch + 512)
            k_, f_ = T.kk[:, cs], PF[ch][:, :]
            fn = pieces("ff", 32 * ch, 32 * ch + 32)
            if s in HALF:
                tt(T.th[:, cs], f_, T.ff[:, cs], A.add, fn, ["#f%d" % ch, "th%d" % ch], 512, 1.0)
                ts(k_, T.th[:, cs], 1.5 * 2 ** 31, 1.5 * 2 ** 31, A.add, A.subtract, ["th%d" % ch], ["kk%d" % ch], 512, 0.5)
                continue
            if s == ST:
                xs(k_, f_, 1.0, -127.5, [], ["#f%d" % ch, "kk%d" % ch], 512)
            else:
                rounder[(s, ch)] = op("X" if ch in PAR["KS"] else "Y", (lambda k_=k_, f_=f_: V.tensor_scalar(k_, f_, 1.5 * 2 ** 31, 1.5 * 2 ** 31, A.add, A.subtract),
                                            lambda k_=k_, f_=f_: S.activation(k_, f_, F.Identity)), [], ["#f%d" % ch, "kk%d" % ch], vc(512))
            tt(T.ff[:, cs], PF[ch][:, :], T.kk[:, cs], A.subtract, ["kk%d" % ch], ["#f%d" % ch] + fn, 512, 1.0)
            if s == ST:
                dma([(T.yf[:, cs], T.ff[:, cs])], fn, [], 131072)

    for s in range(1, ST + 1):
        if s > 1:
            scatter(s - 1, 1)
        if s in CHAIN:
            pass_table(s)
        for b in range(NB):
            choose(s, b)
        if s in CHAIN:
            unfold(s, [])
        if s in (2, 3) and s + 1 not in CHAIN:
            unfold(s + 1, [])
            for s2 in range(1, s):
                scatter(s2, s + 2 - s2)
        winners(s)
        if s < ST:
            scatter(s, 2)
        for q in range(3):
            for b in range(NB):
                letter(s, q, b)
    scatter(ST, 1)
    dma([(T.yent[:, W * c:W * c + W], T.wc[4 * c::16, 0:W]) for c in range(3)] + [(T.yelen[:, :], T.wc[12::16, 0:W])], ["wc"], [], 524288)
    chain = [i for s in range(1, ST + 1) for (b, q) in PAR["ORDER"] for i in gathers[(s, b, q)]]
    for i, j in zip(chain, chain[1:]):
        ops[j]["behind"] = i
    return ops, rloc[0]


def plan(ops):
    nops = len(ops)
    state = [PAR["SEED"] * 7919 + 1]

    def rnd():
        state[0] = (state[0] * 1103515245 + 12345) % 2147483648
        return state[0] / 2147483648.0
    lastw, readers = {}, {}
    pred0 = [dict() for _ in ops]
    for i, o in enumerate(ops):
        if o["after"] is not None:
            pred0[i][o["after"]] = 0
        for w in o["w"]:
            for j in readers.get(w, []) + ([lastw[w]] if w in lastw else []):
                pred0[i][j] = max(pred0[i].get(j, 0), 1 if w[0] == "#" else 2)
        for r in o["r"]:
            if r in lastw:
                pred0[i][lastw[r]] = 2
        for r in o["r"]:
            readers.setdefault(r, []).append(i)
        for w in o["w"]:
            lastw[w] = i
            readers[w] = []
    for i, o in enumerate(ops):
        if o["behind"] is not None and o["behind"] not in pred0[i]:
            pred0[i][o["behind"]] = -1
    succ = [[] for _ in ops]
    for i in range(nops):
        for j in pred0[i]:
            succ[j].append(i)
    line, cnt = [i for i in range(nops) if not pred0[i]], [len(pred0[i]) for i in range(nops)]
    for i in line:
        for k in succ[i]:
            cnt[k] -= 1
            if cnt[k] == 0:
                line.append(k)
    cost, lat, nb = [o["c"] for o in ops], [o["lat"] for o in ops], [o["bytes"] for o in ops]
    LAT, BW, WIN = PAR["LAT"], PAR["BW"], PAR["WIN"]
    level = [0.0] * nops
    for i in line[::-1]:
        level[i] = cost[i] + lat[i] + nb[i] / BW + LAT + max([level[k] for k in succ[i]] + [0.0])

    def greedy(lean, vpen):
        pred = [dict(p) for p in pred0]
        prio = [level[i] + ops[i]["bias"] + lean[i] for i in range(nops)]
        left = [len(p) for p in pred]
        ready = [i for i in range(nops) if left[i] == 0]
        start, done, eng = [0.0] * nops, [0.0] * nops, [o["e"] for o in ops]
        free, base = {e: 0.0 for e in "VSPGQD"}, {}
        users, order = {0: {}, 1: {}}, []
        while ready:
            cand = []
            for i in ready:
                bk = ops[i]["bank"]
                for e in ("VS" if ops[i]["free"] else eng[i]):
                    if (i, e) not in base:
                        t = 0.0
                        for j, k in pred[i].items():
                            if k == -1 or (k == 0 and eng[j] == e):
                                t = max(t, start[j])
                            else:
                                t = max(t, done[j] + (LAT if k == 2 or (k == 1 and eng[j] != e) else 0.0))
                        base[(i, e)] = t
                    t = base[(i, e)] if e == "R" else max(base[(i, e)], free[e])
                    if bk is not None:
                        t = max([t] + [done[j] + LAT for x, j in users[bk].items() if x != e])
                    cand.append((t + (vpen[i] if ops[i]["free"] and e == "V" else 0.0), -prio[i], i, e, t))
            best = min(cand)
            e = best[3]
            if e != "R":
                lim = best[0] + WIN + min(PAR["WIN2"], cost[best[2]] * PAR["WINF"])
                best = min([c for c in cand if c[3] == e and c[0] <= (lim if cost[c[2]] < PAR["SMALL"] else best[0] + WIN)], key=lambda c: c[1])
            i, t = best[2], best[4]
            eng[i] = e
            ready.remove(i)
            order.append(i)
            bk = ops[i]["bank"]
            if bk is not None:
                for j in users[bk].values():
                    pred[i][j] = max(pred[i].get(j, 0), 1)
                users[bk][e] = i
            start[i] = t
            c = cost[i] + (ops[i]["more"] if e == "S" else 0.0)
            if e != "R":
                free[e] = t + c
            done[i] = t + c + lat[i]
            if nb[i]:
                free["D"] = max(free["D"], t + lat[i] / 2) + nb[i] / BW
                done[i] = free["D"] + lat[i] / 2
            for k in succ[i]:
                left[k] -= 1
                if left[k] == 0:
                    ready.append(k)
        hard = [[j for j, k in pred[i].items() if k == 2 or (k == 1 and eng[j] != eng[i]) or eng[i] == "R"] for i in range(nops)]
        return order, hard, eng

    def score(order, hard, eng):
        tot = 0.0
        for cf, gf, sf, df, lf in PAR["VARY"]:
            dn, fr = [0.0] * nops, {e: 0.0 for e in "VSPGQRD"}
            for i in order:
                e = eng[i]
                t = fr[e] if e != "R" else 0.0
                for j in hard[i]:
                    if dn[j] + LAT * lf > t:
                        t = dn[j] + LAT * lf
                kind = ops[i]["kind"]
                t += (cost[i] + (ops[i]["more"] if e == "S" else 0.0)) * cf * (gf if kind == "g" else sf if kind == "s" else 1.0)
                fr[e] = t
                if nb[i]:
                    fr["D"] = max(fr["D"], t + lat[i] * df / 2) + nb[i] / BW * df
                    t = fr["D"] + lat[i] * df / 2
                dn[i] = t
            tot += max(dn) / cf
        return tot / len(PAR["VARY"])

    tags = {}
    for i, o in enumerate(ops):
        tags.setdefault(o["tag"] + o["e"], []).append(i)
    tags = [tags[x] for x in sorted(tags)]
    either = [i for i in range(nops) if ops[i]["free"]]
    lean, vpen = [0.0] * nops, [PAR["VPEN"] if c > 350 else PAR["VP0"] for c in cost]
    keep = None
    for _it in range(PAR["ROUNDS"]):
        l2, v2 = list(lean), list(vpen)
        if keep is not None:
            for _k in range(1 + int(2 * rnd())):
                x = rnd()
                if x < 0.4:
                    d = PAR["JT"] * (rnd() - 0.5)
                    for i in tags[int(rnd() * len(tags))]:
                        l2[i] += d
                elif x < 0.6:
                    l2[int(rnd() * nops)] += PAR["JT"] * (rnd() - 0.5)
                else:
                    i = either[int(rnd() * len(either))]
                    v2[i] = PAR["JG"] * rnd() * (1.0 if cost[i] > 350 else 0.2)
        res = greedy(l2, v2)
        sc = score(*res)
        if keep is None or sc <= now + PAR["TOL"] * rnd() * (1 - _it / PAR["ROUNDS"]):
            now, lean, vpen = sc, l2, v2
        if keep is None or sc <= keep[0]:
            keep = (sc,) + res
    return keep


PLANS = {}


def rank_program(g, core, T, topo):
    rank = T.rank_of(core)
    if rank is None:
        return
    ops, nloc = build(g, T, topo, rank)
    if "plan" not in PLANS:
        PLANS["plan"] = plan(ops)
    _sc, order, hard, engine = PLANS["plan"]
    queues = {"V": g.vector, "S": g.scalar, "P": g.tensor, "Q": g.sync, "G": g}
    need = set()
    for i in range(len(ops)):
        ops[i]["e"] = engine[i]
        for j in hard[i]:
            if ops[j]["sem"] is None:
                need.add(j)
    count = {e: 0 for e in queues}
    mark = {}
    seen = {e: {} for e in queues}
    for i in order:
        o = ops[i]
        e = o["e"]
        if e == "R":
            continue
        waits = {}
        for j in hard[i]:
            if ops[j]["sem"] == "none":
                continue
            if ops[j]["sem"] is None:
                nm, c = "s" + ops[j]["e"], mark[j]
            else:
                nm, c = ops[j]["sem"], ops[j]["cnt"]
            waits[nm] = max(waits.get(nm, 0), c)
        for nm, c in waits.items():
            if seen[e].get(nm, 0) < c:
                queues[e].wait_ge(T.sem[nm], c)
                seen[e][nm] = c
        ins = o["fn"][0 if e == "V" else 1]() if o["free"] else o["fn"]()
        if i in need:
            count[e] += 1
            mark[i] = count[e]
            ins.then_inc(T.sem["s" + e], 1)
    for o in ops:
        if o["sem"] not in (None, "none") and max(seen[e].get(o["sem"], 0) for e in seen) < o["cnt"]:
            g.sync.wait_ge(T.sem[o["sem"]], o["cnt"])
    for e in "VSPG":
        if count[e] and max(seen[x].get("s" + e, 0) for x in seen) < count[e]:
            g.sync.wait_ge(T.sem["s" + e], count[e])
    g.wait_ge(T.sem.rloc, nloc)
